import numpy as np
import ml_dtypes


def mxq(x, axis, fmt="e4m3"):
    dtype, down = {"e4m3": (ml_dtypes.float8_e4m3fn, 7), "e5m2": (ml_dtypes.float8_e5m2, 14)}[fmt]
    v = np.moveaxis(np.asarray(x, np.float32).astype(ml_dtypes.bfloat16).astype(np.float64), axis, -1)
    blocks = v.reshape(v.shape[:-1] + (-1, 32))
    amax = np.abs(blocks).max(-1, keepdims=True)
    byte = np.maximum(np.where(amax > 0, np.frexp(amax)[1] - 1 + 127, 0) - down, 1)
    scale = np.exp2(byte - 127.0)
    codes = (blocks / scale).astype(np.float32).astype(dtype).astype(np.float64)
    return np.moveaxis((codes * scale).reshape(v.shape), -1, axis)


WIDE = False


def mx_kscale(k):
    if not WIDE:
        return np.ones(k)
    levels = np.array([10, -10, 5, -5, 0])
    if k % 512:
        return np.exp2(np.random.permutation(np.resize(levels, k // 32))).repeat(32)
    a = np.empty((k // 512, 16))
    for p in range(k // 512):
        a[p, :8] = np.random.permutation(np.resize(levels, 8))
        for g in range(8):
            far = levels[np.abs(levels - a[p, g]) >= 10]
            a[p, g + 8] = far[np.random.randint(len(far))]
    return np.exp2(a.ravel()).repeat(32)


BF16 = ml_dtypes.bfloat16


def bf(x):
    return np.asarray(x, np.float32).astype(BF16)


def f64(x):
    return np.asarray(x).astype(np.float64)


E2M1 = np.array([0.0, 0.5, 1.0, 1.5, 2.0, 3.0, 4.0, 6.0, -0.0, -0.5, -1.0, -1.5, -2.0, -3.0, -4.0, -6.0])


def pack_weight(w, fmt):
    k, n = w.shape
    w = f64(bf(w)).reshape(k // 32, 32, n)
    amax = np.abs(w).max(1)
    if fmt == "e4m3":
        byte = np.frexp(amax)[1] - 1 + 127 - 7
    else:
        mant, ex = np.frexp(amax / 6.0)
        byte = np.where(mant > 0.5, ex, ex - 1) + 127
    byte = np.clip(np.where(amax > 0, byte, 1), 1, 254)
    scaled = (w * np.exp2(127.0 - byte)[:, None, :]).reshape(k, n).astype(np.float32)
    by_word = np.ascontiguousarray(scaled.reshape(k // 512, 128, 4, n).transpose(0, 1, 3, 2))
    if fmt == "e4m3":
        words = by_word.astype(ml_dtypes.float8_e4m3fn).view(np.uint8)
    else:
        c = by_word.astype(ml_dtypes.float4_e2m1fn).view(np.uint8) & 0xF
        words = c[..., 0::2] | (c[..., 1::2] << 4)
    return np.ascontiguousarray(words), np.ascontiguousarray(byte.astype(np.uint8).reshape(k // 512, 16, n))


def unpack_weight(words, scales, fmt):
    g, p, n, _ = words.shape
    if fmt == "e4m3":
        vals = np.ascontiguousarray(words).view(ml_dtypes.float8_e4m3fn).astype(np.float64)
    else:
        nib = np.empty((g, p, n, 4), np.uint8)
        nib[..., 0::2] = words & 0xF
        nib[..., 1::2] = words >> 4
        vals = E2M1[nib]
    vals = vals * np.repeat(np.exp2(scales.astype(np.float64) - 127.0), 8, axis=1)[..., None]
    return vals.transpose(0, 1, 3, 2).reshape(g * 512, n)
def pack4(w):
    words, scales = pack_weight(w, "e2m1")
    return words.reshape(words.shape[0], 128, -1), scales


def unpack4(words, scales):
    return unpack_weight(words.reshape(words.shape[0], 128, -1, 2), scales, "e2m1")


def planes(Y):
    n, m = Y.shape
    b = f64(bf(Y)).reshape(n // 32, 32, m)
    amax = np.abs(b).max(1)
    byte = np.clip(np.where(amax > 0, np.frexp(amax)[1] - 1 + 127 - 7, 1), 1, 254)
    codes = (b * np.exp2(127.0 - byte)[:, None, :]).reshape(n, m).astype(np.float32).astype(ml_dtypes.float8_e4m3fn).view(np.uint8)
    words = codes.reshape(n // 512, 128, 4, m).transpose(0, 1, 3, 2)
    return np.ascontiguousarray(words), np.ascontiguousarray(byte.astype(np.uint8).reshape(n // 512, 16, m))


M, N, R, L, U = 1024, 1024, 2048, 1024, 1024

def noise(*shape):
    return np.random.randn(*shape)

def setup_inputs():
    s = mx_kscale(R)
    r = mx_kscale(L)
    t = mx_kscale(U)
    codebook_words, codebook_scales = pack4(noise(L, M) * r[:, None])
    return {
        "channel": bf(noise(R, M) * s[:, None]),
        "coef": bf(noise(R, U) / np.sqrt(R) / s[:, None]),
        "codebook_words": codebook_words,
        "codebook_scales": codebook_scales,
        "beam_coef": bf(noise(L, U) / np.sqrt(L) / r[:, None]),
        "user_weight": bf(np.exp(0.4 * noise(U)) * t),
        "precoder2": bf(noise(N, U) / np.sqrt(U) / t[None, :]),
        "gain1": bf(1 + 0.1 * noise(M)),
        "extra": bf(0.5 * noise(M, N)),
        "gain2": bf(np.exp(0.8 * noise(N))),
    }

def reference(channel, coef, codebook_words, codebook_scales, beam_coef, user_weight, precoder2, gain1, extra, gain2):
    h = mxq(f64(channel), 0)
    x = mxq(f64(coef), 0)
    c = unpack4(codebook_words, codebook_scales)
    d = mxq(f64(beam_coef), 0)
    v1 = (h.T @ x) + (c.T @ d)
    vw = v1 * f64(user_weight)[None, :]
    v2 = mxq(f64(precoder2), 1)
    cov = mxq(vw, 1) @ v2.T
    y = (cov * f64(gain1)[:, None] + f64(extra)) * f64(gain2)[None, :]
    Y = y.T
    words, scales = planes(Y)
    return y, words, scales

@@ -1,0 +1,625 @@
+from contextlib import ExitStack
+
+import concourse.mybir as mybir
+from concourse.masks import make_identity
+
+M, N, R, L, U = 1024, 1024, 2048, 1024, 1024
+FLOPS = 2 * M * U * (R + L) + 2 * M * N * U
+
+F32 = mybir.dt.float32
+BF16 = mybir.dt.bfloat16
+U32 = mybir.dt.uint32
+I32 = mybir.dt.int32
+U8 = mybir.dt.uint8
+FP8X4 = mybir.dt.float8_e4m3fn_x4
+FP4X4 = mybir.dt.float4_e2m1fn_x4
+COPY = mybir.ActivationFunctionType.Copy
+MULT = mybir.AluOpType.mult
+ADD = mybir.AluOpType.add
+
+P = 128
+HALF = 512
+PASSES = [("h", 0), ("h", 1), ("h", 2), ("h", 3), ("c", 0), ("c", 1)]
+GROUPED_BUFS = 7
+WIDE_BUFS = 4
+NARROW_BUFS = 6
+VW_BUFS = 2
+Y_BUFS = 6
+SUM_BUFS = 4
+RND_BUFS = 5
+GY_BUFS = 4
+WIDE_OUT = "p (t m j) -> p m j t"
+WIDE_IN = "p j (m t) -> p m j t"
+WB1 = "SSSS"
+
+
+def tile_weighted_transmit_covariance_block_k6_kernel(
+    tc, channel, coef, codebook_words, codebook_scales, beam_coef, user_weight, precoder2, gain1, extra, gain2,
+    out_0, out_1, out_2,
+):
+    nc = tc.nc
+    with ExitStack() as ctx:
+        keep = ctx.enter_context(tc.tile_pool(name="keep", bufs=1))
+        stage = ctx.enter_context(tc.tile_pool(name="stage", bufs=1))
+        psum = ctx.enter_context(tc.psum_pool(name="psum", bufs=1))
+        ctx.enter_context(tc.manual_schedule())
+        T = {}
+
+        def bank(b, shape, dtype, name):
+            return psum.tile(shape, dtype, name=name, tag="bank%d" % b)
+
+        def quantised(name, width):
+            codes = keep.tile([P, width], U32, name=name + "_codes", align_bytes=64)
+            scales = keep.tile([P, width], U8, name=name + "_scales", align_bytes=64)
+            return codes, scales
+
+        def grouped_tile(name):
+            return stage.tile([P, 4 * HALF], BF16, name=name, tag="grouped", bufs=GROUPED_BUFS, align_bytes=64)
+
+        def copy_on(engine, out, in_):
+            if engine == "V":
+                nc.vector.tensor_copy(out=out, in_=in_)
+            else:
+                nc.scalar.copy(out=out, in_=in_)
+
+        def quantise(pair, cols, source):
+            codes, scales = pair
+            nc.vector.quantize_mx(out=codes[:, cols].bitcast(FP8X4), scales=scales[:, cols], in_=source)
+
+        def load_wide(s):
+            kind, k = PASSES[s]
+            src = coef if kind == "h" else beam_coef
+            raw = stage.tile([P, 4, U], BF16, name="wide%d" % s, tag="wide", bufs=WIDE_BUFS)
+            nc.sync.dma_start(out=raw[:], in_=src[HALF * k : HALF * (k + 1), :].rearrange("(p j) u -> p j u", j=4))
+            T["wide", s] = raw
+
+        def load_channel(s, mh):
+            k = PASSES[s][1]
+            raw = stage.tile([P, 4, HALF], BF16, name="chan%d_%d" % (s, mh), tag="narrow", bufs=NARROW_BUFS)
+            rows = channel[HALF * k : HALF * (k + 1), HALF * mh : HALF * (mh + 1)]
+            nc.sync.dma_start(out=raw[:], in_=rows.rearrange("(p j) m -> p j m", j=4))
+            T["chan", s, mh] = raw
+
+        def load_codebook(k):
+            nc.sync.dma_start(out=book_words[:, k, :].bitcast(I32), in_=codebook_words[k].bitcast(I32))
+
+        def load_precoder(nh):
+            raw = stage.tile([P, 4, U], BF16, name="prec%d" % nh, tag="wide", bufs=WIDE_BUFS)
+            nc.sync.dma_start(out=raw[:], in_=precoder2[HALF * nh : HALF * (nh + 1), :].rearrange("(j p) u -> p j u", p=P))
+            T["prec", nh] = raw
+
+        def load_extra(mh, nh):
+            raw = stage.tile([P, 4, HALF], BF16, name="extra%d_%d" % (mh, nh), tag="narrow", bufs=NARROW_BUFS)
+            rows = extra[HALF * mh : HALF * (mh + 1), HALF * nh : HALF * (nh + 1)]
+            nc.sync.dma_start(out=raw[:], in_=rows.rearrange("(j p) n -> p j n", p=P))
+            T["extra", mh, nh] = raw
+
+        def group_wide(s, g, engine):
+            grouped = grouped_tile("gw%d_%d" % (s, g))
+            copy_on(
+                engine,
+                grouped[:].rearrange(WIDE_OUT, t=4, j=4),
+                T["wide", s][:, :, HALF * g : HALF * (g + 1)].rearrange(WIDE_IN, t=4),
+            )
+            T["gw", s, g] = grouped
+
+        def quant_wide(s, g):
+            T["qw", s, g] = quantised("qw%d_%d" % (s, g), HALF)
+            quantise(T["qw", s, g], slice(0, HALF), T["gw", s, g][:])
+
+        def interleave(engine, grouped, rows, lo, hi):
+            copy_on(
+                engine,
+                grouped[:, 4 * lo : 4 * hi].rearrange("p (c i j) -> p c j i", i=4, j=4),
+                rows[:, :, lo:hi].rearrange("p j (c i) -> p c j i", i=4),
+            )
+
+        def group_channel(s, mh, engine, lo, hi):
+            if ("gc", s, mh) not in T:
+                T["gc", s, mh] = grouped_tile("gc%d_%d" % (s, mh))
+            interleave(engine, T["gc", s, mh], T["chan", s, mh], lo, hi)
+
+        def quant_channel(s, mh):
+            T["qc", s, mh] = quantised("qc%d_%d" % (s, mh), HALF)
+            quantise(T["qc", s, mh], slice(0, HALF), T["gc", s, mh][:])
+
+        def stage1(s, mh, g, t, b):
+            kind, k = PASSES[s]
+            done = T.get(("passes", mh, g, t), 0)
+            T["passes", mh, g, t] = done + 1
+            if done == 0:
+                T["acc1", mh, g, t] = bank(b, [P, HALF], F32, "acc1_%d_%d_%d" % (mh, g, t))
+            codes, scales = T["qw", s, g]
+            cols = slice(P * t, P * (t + 1))
+            if kind == "h":
+                rhs = T["qc", s, mh][0][:].bitcast(FP8X4)
+                rhs_scale = T["qc", s, mh][1][:]
+            else:
+                rhs = book_words[:, k, 2 * HALF * mh : 2 * HALF * (mh + 1)].bitcast(FP4X4)
+                rhs_scale = book_scales[:, k, HALF * mh : HALF * (mh + 1)]
+            nc.tensor.matmul_mx(
+                out=T["acc1", mh, g, t][:], lhsT=codes[:, cols].bitcast(FP8X4), lhsT_scale=scales[:, cols],
+                rhs=rhs, rhs_scale=rhs_scale, start=(done == 0), stop=(done == len(PASSES) - 1),
+            )
+
+        def weigh(mh, g, t, engine):
+            if ("vw", mh, g) not in T:
+                T["vw", mh, g] = stage.tile([P, 4, HALF], BF16, name="vw%d_%d" % (mh, g), tag="vw", bufs=VW_BUFS)
+            out = T["vw", mh, g][:, t, :]
+            weight = weights[:, 4 * g + t : 4 * g + t + 1]
+            if engine == "V":
+                nc.vector.tensor_scalar(out=out, in0=T["acc1", mh, g, t][:], scalar1=weight, scalar2=None, op0=MULT)
+            else:
+                nc.scalar.activation(out=out, in_=T["acc1", mh, g, t][:], func=COPY, scale=weight)
+
+        def group_vw(mh, g, engine, lo, hi):
+            if ("gv", mh, g) not in T:
+                T["gv", mh, g] = grouped_tile("gv%d_%d" % (mh, g))
+            interleave(engine, T["gv", mh, g], T["vw", mh, g], lo, hi)
+
+        def quant_vw(mh, g):
+            T["qv", mh, g] = quantised("qv%d_%d" % (mh, g), HALF)
+            quantise(T["qv", mh, g], slice(0, HALF), T["gv", mh, g][:])
+
+        def turn_precoder(nh, g, jj, b):
+            words = T["prec", nh][:].bitcast(F32)
+            turned = bank(b, [P, 2, 2, P], F32, "pt%d_%d_%d" % (nh, g, jj))
+            for j in range(2):
+                for h in range(2):
+                    nc.tensor.transpose(turned[:, j, h, :], words[:, 2 * jj + j, 256 * g + h : 256 * (g + 1) : 2], ident_f32[:])
+            T["pt", nh, g, jj] = turned
+
+        def group_precoder(nh, g, jj, engine):
+            if ("gp", nh, g) not in T:
+                T["gp", nh, g] = grouped_tile("gp%d_%d" % (nh, g))
+            out = T["gp", nh, g][:].bitcast(F32)[:, HALF * jj : HALF * (jj + 1)].rearrange("p (j r h) -> p j r h", j=2, h=2)
+            copy_on(engine, out, T["pt", nh, g, jj][:].rearrange("p j h r -> p j r h"))
+
+        def quant_precoder(nh, g):
+            T["qp", nh, g] = quantised("qp%d_%d" % (nh, g), HALF)
+            quantise(T["qp", nh, g], slice(0, HALF), T["gp", nh, g][:])
+
+        def stage2(mt, nh, b):
+            acc = bank(b, [P, HALF], F32, "acc2_%d_%d" % (mt, nh))
+            cols = slice(P * (mt % 4), P * (mt % 4 + 1))
+            for g in range(2):
+                codes, scales = T["qv", mt // 4, g]
+                nc.tensor.matmul_mx(
+                    out=acc[:], lhsT=codes[:, cols].bitcast(FP8X4), lhsT_scale=scales[:, cols],
+                    rhs=T["qp", nh, g][0][:].bitcast(FP8X4), rhs_scale=T["qp", nh, g][1][:],
+                    start=(g == 0), stop=(g == 1),
+                )
+            T["acc2", mt, nh] = acc
+
+        def add_extra(mt, nh):
+            summed = stage.tile([P, HALF], F32, name="sum%d_%d" % (mt, nh), tag="summed", bufs=SUM_BUFS)
+            nc.vector.scalar_tensor_tensor(
+                out=summed[:], in0=T["acc2", mt, nh][:], scalar=gain1_cols[:, mt : mt + 1],
+                in1=T["extra", mt // 4, nh][:, mt % 4, :], op0=MULT, op1=ADD,
+            )
+            T["sum", mt, nh] = summed
+
+        def finish_y(mt, nh):
+            y = stage.tile([P, HALF], F32, name="y%d_%d" % (mt, nh), tag="y", bufs=Y_BUFS)
+            nc.vector.tensor_tensor(out=y[:], in0=T["sum", mt, nh][:], in1=gain2_rows[:, HALF * nh : HALF * (nh + 1)], op=MULT)
+            T["y", mt, nh] = y
+
+        def store_y(mt, nh):
+            nc.sync.dma_start(out=out_0[P * mt : P * (mt + 1), HALF * nh : HALF * (nh + 1)], in_=T["y", mt, nh][:])
+
+        def round_y(mt, nh, engine):
+            rounded = stage.tile([P, HALF], BF16, name="yb%d_%d" % (mt, nh), tag="rounded", bufs=RND_BUFS)
+            copy_on(engine, rounded[:].rearrange("m (h p e) -> m h p e", h=2, e=2), T["y", mt, nh][:].rearrange("m (p h e) -> m h p e", h=2, e=2))
+            T["yb", mt, nh] = rounded
+
+        def turn_y(mt0, count, nh, b):
+            turned = bank(b, [P, count, 2, P], F32, "yt%d_%d" % (mt0, nh))
+            for i in range(count):
+                words = T["yb", mt0 + i, nh][:].bitcast(F32)
+                for h in range(2):
+                    nc.tensor.transpose(turned[:, i, h, :], words[:, P * h : P * (h + 1)], ident_f32[:])
+            T["yt", mt0, nh] = turned
+
+        def group_y(mt0, count, nh, engine):
+            grouped = stage.tile([P, 4 * P * count], BF16, name="gy%d_%d" % (mt0, nh), tag="grouped_y", bufs=GY_BUFS, align_bytes=64)
+            copy_on(engine, grouped[:].bitcast(F32).rearrange("p (i m h) -> p i m h", i=count, h=2), T["yt", mt0, nh][:].rearrange("p i h m -> p i m h"))
+            T["gy", mt0, nh] = grouped
+
+        def quant_y(mt0, count, nh):
+            cols = slice(P * (mt0 % 4), P * (mt0 % 4 + count))
+            codes, scales = y_planes[mt0 // 4]
+            nc.vector.quantize_mx(out=codes[:, nh, cols].bitcast(FP8X4), scales=scales[:, nh, cols], in_=T["gy", mt0, nh][:])
+
+        def store_codes(mt0, count, nh):
+            words = out_1[nh].rearrange("p m t -> p (m t)").bitcast(I32)
+            cols = slice(P * (mt0 % 4), P * (mt0 % 4 + count))
+            nc.sync.dma_start(out=words[:, P * mt0 : P * (mt0 + count)], in_=y_planes[mt0 // 4][0][:, nh, cols].bitcast(I32))
+
+        def store_scales(mh, queues):
+            for q in range(4):
+                queues[q].dma_start(
+                    out=out_2[:, 4 * q : 4 * q + 4, HALF * mh : HALF * (mh + 1)].bitcast(I32).rearrange("g r c -> r g c"),
+                    in_=y_planes[mh][1][32 * q : 32 * q + 4, :, :].bitcast(I32),
+                )
+
+        book_words = keep.tile([P, 2, 2 * M], U8, name="book_words", align_bytes=64)
+        book_scales = keep.tile([P, 2, M], U8, name="book_scales", align_bytes=64)
+        y_planes = []
+        for mh in range(2):
+            codes = keep.tile([P, 2, HALF], U32, name="y_codes%d" % mh, align_bytes=64)
+            scales = keep.tile([P, 2, HALF], U8, name="y_scales%d" % mh, align_bytes=64)
+            y_planes.append((codes, scales))
+        ident_f32 = keep.tile([P, P], F32, name="ident_f32")
+        ident_bf16 = keep.tile([P, P], BF16, name="ident_bf16")
+        gain_rows = keep.tile([P, P], BF16, name="gain_rows")
+        gain1_cols = keep.tile([P, 8], F32, name="gain1_cols")
+        gain2_cols = keep.tile([P, 8], BF16, name="gain2_cols")
+        gain2_rows = keep.tile([P, N], BF16, name="gain2_rows")
+        weights_bf16 = keep.tile([P, 2, 4], BF16, name="weights_bf16")
+        weights = keep.tile([P, 8], F32, name="weights")
+
+        nc.vector.memset(gain_rows[:].bitcast(I32), 0)
+        nc.vector.memset(book_scales[:].bitcast(I32), 0)
+        make_identity(nc, ident_f32[:])
+        nc.scalar.dma_start(out=gain_rows[0:8, :], in_=gain1.rearrange("(j p) -> j p", p=P))
+        nc.scalar.dma_start(out=gain_rows[8:16, :], in_=gain2.rearrange("(j p) -> j p", p=P))
+        nc.scalar.dma_start(out=weights_bf16[:], in_=user_weight.rearrange("(g p t) -> p g t", g=2, t=4))
+        for q in range(4):
+            nc.gpsimd.dma_start(
+                out=book_scales[32 * q : 32 * q + 4, :, :].bitcast(I32),
+                in_=codebook_scales[:, 4 * q : 4 * q + 4, :].bitcast(I32).rearrange("g r c -> r g c"),
+            )
+        nc.scalar.activation(out=ident_bf16[:], in_=ident_f32[:], func=COPY)
+
+        def gains_turn(b):
+            T["gain_cols"] = bank(b, [P, P], BF16, "gain_cols")
+            nc.tensor.transpose(T["gain_cols"][:], gain_rows[:], ident_bf16[:])
+
+        def gains_cols():
+            nc.vector.tensor_copy(out=gain2_cols[:], in_=T["gain_cols"][:, 8:16])
+            nc.vector.tensor_copy(out=gain1_cols[:], in_=T["gain_cols"][:, 0:8])
+            nc.vector.tensor_copy(out=weights[:], in_=weights_bf16[:].rearrange("p g t -> p (g t)"))
+
+        def gains_spread(b):
+            T["spread"] = bank(b, [P, N], BF16, "spread")
+            for j in range(8):
+                nc.tensor.transpose(T["spread"][:, P * j : P * (j + 1)], gain2_cols[:, j : j + 1].to_broadcast([P, P]), ident_bf16[:])
+
+        def gains_rows():
+            nc.scalar.copy(out=gain2_rows[:], in_=T["spread"][:])
+
+        gains_turn(0)
+        gains_cols()
+        load_channel(0, 0)
+        group_channel(0, 0, "S", 0, 256)
+        group_channel(0, 0, "V", 256, 512)
+        gains_spread(1)
+        quant_channel(0, 0)
+        load_wide(0)
+        group_wide(0, 0, "V")
+        quant_wide(0, 0)
+        gains_rows()
+        stage1(0, 0, 0, 2, 2)
+        load_wide(1)
+        group_wide(1, 0, "V")
+        load_channel(1, 0)
+        group_wide(0, 1, "S")
+        quant_wide(0, 1)
+        group_channel(1, 0, "V", 256, 512)
+        quant_wide(1, 0)
+        group_wide(1, 1, "S")
+        quant_wide(1, 1)
+        group_channel(1, 0, "S", 0, 256)
+        stage1(0, 0, 1, 3, 3)
+        stage1(0, 0, 1, 1, 4)
+        quant_channel(1, 0)
+        stage1(1, 0, 1, 2, 5)
+        load_wide(2)
+        group_wide(2, 0, "V")
+        stage1(0, 0, 1, 0, 6)
+        stage1(1, 0, 1, 1, 4)
+        load_channel(2, 0)
+        group_wide(2, 1, "S")
+        group_channel(2, 0, "V", 0, 256)
+        stage1(1, 0, 0, 0, 7)
+        quant_wide(2, 0)
+        quant_wide(2, 1)
+        stage1(1, 0, 0, 1, 0)
+        group_channel(2, 0, "S", 256, 512)
+        stage1(1, 0, 0, 2, 2)
+        stage1(1, 0, 0, 3, 1)
+        stage1(1, 0, 1, 0, 6)
+        quant_channel(2, 0)
+        stage1(2, 0, 1, 2, 5)
+        stage1(2, 0, 0, 0, 7)
+        stage1(2, 0, 0, 1, 0)
+        stage1(2, 0, 0, 2, 2)
+        stage1(0, 0, 1, 2, 5)
+        stage1(2, 0, 1, 1, 4)
+        stage1(2, 0, 1, 3, 3)
+        stage1(2, 0, 0, 3, 1)
+        stage1(1, 0, 1, 3, 3)
+        stage1(0, 0, 0, 3, 1)
+        stage1(0, 0, 0, 1, 0)
+        load_channel(3, 0)
+        group_channel(3, 0, "V", 256, 512)
+        group_channel(3, 0, "S", 0, 256)
+        load_wide(3)
+        group_wide(3, 0, "V")
+        load_wide(4)
+        quant_channel(3, 0)
+        stage1(0, 0, 0, 0, 7)
+        load_wide(5)
+        stage1(2, 0, 1, 0, 6)
+        quant_wide(3, 0)
+        stage1(3, 0, 0, 3, 1)
+        stage1(3, 0, 0, 2, 2)
+        stage1(3, 0, 0, 0, 7)
+        stage1(3, 0, 0, 1, 0)
+        group_wide(4, 1, "V")
+        group_wide(3, 1, "S")
+        quant_wide(3, 1)
+        stage1(3, 0, 1, 2, 5)
+        stage1(3, 0, 1, 0, 6)
+        load_codebook(0)
+        stage1(3, 0, 1, 1, 4)
+        quant_wide(4, 1)
+        stage1(4, 0, 1, 2, 5)
+        stage1(4, 0, 1, 1, 4)
+        stage1(4, 0, 1, 0, 6)
+        load_codebook(1)
+        group_wide(4, 0, "S")
+        quant_wide(4, 0)
+        stage1(4, 0, 0, 0, 7)
+        stage1(4, 0, 0, 1, 0)
+        stage1(3, 0, 1, 3, 3)
+        stage1(4, 0, 0, 2, 2)
+        group_wide(5, 0, "V")
+        quant_wide(5, 0)
+        stage1(4, 0, 0, 3, 1)
+        load_channel(3, 1)
+        group_wide(5, 1, "S")
+        quant_wide(5, 1)
+        stage1(4, 0, 1, 3, 3)
+        group_channel(3, 1, "S", 256, 512)
+        stage1(5, 0, 0, 3, 1)
+        weigh(0, 0, 3, "S")
+        stage1(5, 0, 0, 0, 7)
+        stage1(5, 0, 0, 1, 0)
+        stage1(5, 0, 1, 2, 5)
+        stage1(5, 0, 1, 3, 3)
+        weigh(0, 0, 1, "S")
+        load_channel(1, 1)
+        stage1(5, 0, 1, 0, 6)
+        group_channel(3, 1, "V", 0, 256)
+        stage1(5, 0, 0, 2, 2)
+        weigh(0, 1, 3, "S")
+        group_channel(1, 1, "V", 0, 256)
+        load_channel(2, 1)
+        stage1(4, 1, 1, 3, 1)
+        weigh(0, 0, 0, "S")
+        stage1(5, 0, 1, 1, 4)
+        stage1(4, 1, 1, 1, 0)
+        quant_channel(3, 1)
+        stage1(4, 1, 1, 2, 3)
+        stage1(3, 1, 1, 2, 3)
+        stage1(3, 1, 1, 1, 0)
+        group_channel(2, 1, "S", 256, 512)
+        weigh(0, 0, 2, "S")
+        group_channel(1, 1, "V", 256, 512)
+        quant_channel(1, 1)
+        stage1(1, 1, 1, 0, 7)
+        stage1(3, 1, 1, 3, 1)
+        stage1(1, 1, 1, 2, 3)
+        group_channel(2, 1, "V", 0, 256)
+        stage1(1, 1, 1, 1, 0)
+        stage1(3, 1, 1, 0, 7)
+        quant_channel(2, 1)
+        load_channel(0, 1)
+        stage1(2, 1, 1, 1, 0)
+        stage1(2, 1, 1, 0, 7)
+        load_precoder(0)
+        stage1(2, 1, 1, 3, 1)
+        stage1(2, 1, 1, 2, 3)
+        stage1(4, 1, 1, 0, 7)
+        group_vw(0, 0, "V", 256, 512)
+        weigh(0, 1, 1, "V")
+        stage1(5, 1, 1, 1, 0)
+        weigh(0, 1, 2, "S")
+        stage1(5, 1, 1, 3, 1)
+        turn_precoder(0, 1, 0, 2)
+        weigh(0, 1, 0, "S")
+        group_vw(0, 1, "S", 0, 256)
+        group_vw(0, 0, "V", 0, 256)
+        group_vw(0, 1, "V", 256, 512)
+        quant_vw(0, 0)
+        group_channel(0, 1, "V", 0, 256)
+        group_precoder(0, 1, 0, "S")
+        turn_precoder(0, 0, 0, 5)
+        group_precoder(0, 0, 0, "S")
+        turn_precoder(0, 0, 1, 6)
+        turn_precoder(0, 1, 1, 4)
+        group_channel(0, 1, "V", 256, 512)
+        group_precoder(0, 1, 1, "S")
+        group_precoder(0, 0, 1, "S")
+        quant_vw(0, 1)
+        quant_channel(0, 1)
+        load_precoder(1)
+        turn_precoder(1, 0, 0, 2)
+        turn_precoder(1, 1, 0, 5)
+        group_precoder(1, 1, 0, "S")
+        turn_precoder(1, 1, 1, 4)
+        group_precoder(1, 1, 1, "S")
+        quant_precoder(0, 1)
+        turn_precoder(1, 0, 1, 6)
+        stage1(0, 1, 1, 1, 0)
+        group_precoder(1, 0, 1, "S")
+        quant_precoder(0, 0)
+        group_precoder(1, 0, 0, "V")
+        weigh(1, 1, 1, "S")
+        quant_precoder(1, 1)
+        load_extra(1, 1)
+        stage1(0, 1, 1, 3, 1)
+        stage1(1, 1, 1, 3, 1)
+        weigh(1, 1, 3, "S")
+        load_extra(0, 0)
+        stage2(2, 0, 5)
+        stage2(3, 0, 4)
+        stage1(0, 1, 0, 1, 2)
+        quant_precoder(1, 0)
+        stage2(3, 1, 6)
+        add_extra(2, 0)
+        add_extra(3, 0)
+        finish_y(3, 0)
+        load_extra(0, 1)
+        round_y(3, 0, "S")
+        store_y(3, 0)
+        stage2(2, 1, 0)
+        add_extra(2, 1)
+        stage1(5, 1, 1, 2, 3)
+        finish_y(2, 0)
+        round_y(2, 0, "S")
+        stage2(0, 0, 1)
+        stage1(5, 1, 1, 0, 7)
+        stage1(0, 1, 1, 0, 7)
+        weigh(1, 1, 0, "S")
+        stage2(1, 1, 5)
+        load_extra(1, 0)
+        stage1(0, 1, 1, 2, 3)
+        weigh(1, 1, 2, "S")
+        stage1(0, 1, 0, 3, 4)
+        group_vw(1, 1, "S", 256, 512)
+        stage1(4, 1, 0, 2, 0)
+        add_extra(3, 1)
+        finish_y(3, 1)
+        store_y(3, 1)
+        add_extra(1, 1)
+        finish_y(2, 1)
+        store_y(2, 0)
+        finish_y(1, 1)
+        stage2(0, 1, 6)
+        stage1(4, 1, 0, 3, 4)
+        add_extra(0, 1)
+        round_y(1, 1, "S")
+        stage1(0, 1, 0, 0, 7)
+        round_y(2, 1, "S")
+        stage1(4, 1, 0, 0, 7)
+        add_extra(0, 0)
+        finish_y(0, 0)
+        stage1(4, 1, 0, 1, 2)
+        stage1(1, 1, 0, 3, 4)
+        store_y(2, 1)
+        stage2(1, 0, 3)
+        add_extra(1, 0)
+        stage1(2, 1, 0, 3, 4)
+        finish_y(0, 1)
+        turn_y(2, 2, 0, 5)
+        group_y(2, 2, 0, "S")
+        quant_y(2, 2, 0)
+        stage1(2, 1, 0, 0, 7)
+        store_codes(2, 2, 0)
+        finish_y(1, 0)
+        round_y(0, 1, "V")
+        stage1(3, 1, 0, 0, 7)
+        round_y(0, 0, "S")
+        stage1(5, 1, 0, 1, 2)
+        stage1(1, 1, 0, 0, 7)
+        stage1(1, 1, 0, 1, 2)
+        stage1(2, 1, 0, 1, 2)
+        stage1(5, 1, 0, 3, 4)
+        store_y(0, 1)
+        store_y(1, 1)
+        stage1(5, 1, 0, 0, 7)
+        group_vw(1, 1, "S", 0, 256)
+        quant_vw(1, 1)
+        stage1(1, 1, 0, 2, 0)
+        weigh(1, 0, 0, "S")
+        store_y(1, 0)
+        stage1(3, 1, 0, 1, 2)
+        weigh(1, 0, 1, "V")
+        round_y(3, 1, "V")
+        stage1(3, 1, 0, 3, 4)
+        weigh(1, 0, 3, "S")
+        stage1(0, 1, 0, 2, 0)
+        stage1(2, 1, 0, 2, 0)
+        stage1(5, 1, 0, 2, 0)
+        stage1(3, 1, 0, 2, 0)
+        weigh(1, 0, 2, "V")
+        turn_y(0, 2, 1, 6)
+        group_vw(1, 0, "S", 0, 256)
+        group_y(0, 2, 1, "S")
+        group_vw(1, 0, "V", 256, 512)
+        quant_vw(1, 0)
+        turn_y(2, 2, 1, 1)
+        stage2(7, 0, 5)
+        stage2(6, 0, 3)
+        quant_y(0, 2, 1)
+        group_y(2, 2, 1, "S")
+        quant_y(2, 2, 1)
+        store_y(0, 0)
+        add_extra(7, 0)
+        add_extra(6, 0)
+        finish_y(7, 0)
+        store_y(7, 0)
+        store_codes(2, 2, 1)
+        round_y(1, 0, "S")
+        finish_y(6, 0)
+        store_y(6, 0)
+        turn_y(0, 2, 0, 7)
+        group_y(0, 2, 0, "S")
+        stage2(4, 0, 4)
+        add_extra(4, 0)
+        stage2(4, 1, 2)
+        add_extra(4, 1)
+        finish_y(4, 0)
+        quant_y(0, 2, 0)
+        stage2(5, 1, 0)
+        add_extra(5, 1)
+        finish_y(4, 1)
+        stage2(5, 0, 6)
+        finish_y(5, 1)
+        store_codes(0, 2, 1)
+        store_y(4, 1)
+        store_codes(0, 2, 0)
+        stage2(6, 1, 1)
+        round_y(6, 0, "S")
+        store_y(5, 1)
+        round_y(7, 0, "S")
+        store_y(4, 0)
+        add_extra(6, 1)
+        round_y(4, 0, "S")
+        turn_y(6, 2, 0, 5)
+        add_extra(5, 0)
+        store_scales(0, [nc.sync] * 4)
+        finish_y(6, 1)
+        store_y(6, 1)
+        round_y(4, 1, "S")
+        stage2(7, 1, 3)
+        round_y(5, 1, "S")
+        group_y(6, 2, 0, "S")
+        finish_y(5, 0)
+        store_y(5, 0)
+        add_extra(7, 1)
+        quant_y(6, 2, 0)
+        store_codes(6, 2, 0)
+        round_y(6, 1, "S")
+        turn_y(4, 2, 1, 7)
+        finish_y(7, 1)
+        store_y(7, 1)
+        round_y(5, 0, "S")
+        turn_y(4, 2, 0, 4)
+        group_y(4, 2, 1, "S")
+        turn_y(6, 1, 1, 2)
+        group_y(6, 1, 1, "S")
+        round_y(7, 1, "V")
+        turn_y(7, 1, 1, 0)
+        quant_y(6, 1, 1)
+        quant_y(4, 2, 1)
+        group_y(4, 2, 0, "S")
+        quant_y(4, 2, 0)
+        store_codes(4, 2, 0)
+        group_y(7, 1, 1, "S")
+        quant_y(7, 1, 1)
+        store_codes(4, 2, 1)
+        store_scales(1, [nc.sync] * 4)
+        store_codes(6, 2, 1)

@@ -258,11 +258,11 @@ def tile_weighted_transmit_covariance_block_k6_kernel(
         weights_bf16 = keep.tile([P, 2, 4], BF16, name="weights_bf16")
         weights = keep.tile([P, 8], F32, name="weights")
 
+        nc.sync.dma_start(out=gain2_cols[:], in_=gain2.rearrange("(p j) -> p j", j=8))
         nc.vector.memset(gain_rows[:].bitcast(I32), 0)
         nc.vector.memset(book_scales[:].bitcast(I32), 0)
         make_identity(nc, ident_f32[:])
         nc.scalar.dma_start(out=gain_rows[0:8, :], in_=gain1.rearrange("(j p) -> j p", p=P))
-        nc.scalar.dma_start(out=gain_rows[8:16, :], in_=gain2.rearrange("(j p) -> j p", p=P))
         nc.scalar.dma_start(out=weights_bf16[:], in_=user_weight.rearrange("(g p t) -> p g t", g=2, t=4))
         for q in range(4):
             nc.gpsimd.dma_start(
@@ -276,8 +276,9 @@ def tile_weighted_transmit_covariance_block_k6_kernel(
             nc.tensor.transpose(T["gain_cols"][:], gain_rows[:], ident_bf16[:])
 
         def gains_cols():
-            nc.vector.tensor_copy(out=gain2_cols[:], in_=T["gain_cols"][:, 8:16])
             nc.vector.tensor_copy(out=gain1_cols[:], in_=T["gain_cols"][:, 0:8])
+
+        def widen_weights():
             nc.vector.tensor_copy(out=weights[:], in_=weights_bf16[:].rearrange("p g t -> p (g t)"))
 
         def gains_spread(b):
@@ -286,340 +287,341 @@ def tile_weighted_transmit_covariance_block_k6_kernel(
                 nc.tensor.transpose(T["spread"][:, P * j : P * (j + 1)], gain2_cols[:, j : j + 1].to_broadcast([P, P]), ident_bf16[:])
 
         def gains_rows():
-            nc.scalar.copy(out=gain2_rows[:], in_=T["spread"][:])
+            nc.scalar.copy(out=gain2_rows[:].rearrange("q (p j) -> q p j", j=8), in_=T["spread"][:].rearrange("q (j p) -> q p j", j=8))
 
-        gains_turn(0)
-        gains_cols()
         load_channel(0, 0)
-        group_channel(0, 0, "S", 0, 256)
+        group_channel(0, 0, "V", 0, 256)
         group_channel(0, 0, "V", 256, 512)
-        gains_spread(1)
-        quant_channel(0, 0)
         load_wide(0)
+        quant_channel(0, 0)
+        gains_spread(0)
+        gains_rows()
         group_wide(0, 0, "V")
         quant_wide(0, 0)
-        gains_rows()
+        stage1(0, 0, 0, 0, 1)
         stage1(0, 0, 0, 2, 2)
+        stage1(0, 0, 0, 1, 3)
+        stage1(0, 0, 0, 3, 4)
         load_wide(1)
         group_wide(1, 0, "V")
+        quant_wide(1, 0)
         load_channel(1, 0)
         group_wide(0, 1, "S")
         quant_wide(0, 1)
-        group_channel(1, 0, "V", 256, 512)
-        quant_wide(1, 0)
+        stage1(0, 0, 1, 0, 5)
+        stage1(0, 0, 1, 3, 6)
         group_wide(1, 1, "S")
         quant_wide(1, 1)
-        group_channel(1, 0, "S", 0, 256)
-        stage1(0, 0, 1, 3, 3)
-        stage1(0, 0, 1, 1, 4)
+        stage1(0, 0, 1, 2, 7)
+        group_channel(1, 0, "V", 0, 256)
+        group_channel(1, 0, "S", 256, 512)
         quant_channel(1, 0)
-        stage1(1, 0, 1, 2, 5)
+        stage1(1, 0, 1, 0, 5)
+        stage1(1, 0, 1, 3, 6)
+        stage1(1, 0, 1, 1, 0)
         load_wide(2)
-        group_wide(2, 0, "V")
-        stage1(0, 0, 1, 0, 6)
-        stage1(1, 0, 1, 1, 4)
-        load_channel(2, 0)
         group_wide(2, 1, "S")
+        group_wide(2, 0, "V")
+        load_channel(2, 0)
+        stage1(0, 0, 1, 1, 0)
         group_channel(2, 0, "V", 0, 256)
-        stage1(1, 0, 0, 0, 7)
-        quant_wide(2, 0)
-        quant_wide(2, 1)
-        stage1(1, 0, 0, 1, 0)
         group_channel(2, 0, "S", 256, 512)
-        stage1(1, 0, 0, 2, 2)
-        stage1(1, 0, 0, 3, 1)
-        stage1(1, 0, 1, 0, 6)
+        quant_wide(2, 1)
+        quant_wide(2, 0)
+        stage1(1, 0, 1, 2, 7)
         quant_channel(2, 0)
-        stage1(2, 0, 1, 2, 5)
-        stage1(2, 0, 0, 0, 7)
-        stage1(2, 0, 0, 1, 0)
-        stage1(2, 0, 0, 2, 2)
-        stage1(0, 0, 1, 2, 5)
-        stage1(2, 0, 1, 1, 4)
-        stage1(2, 0, 1, 3, 3)
-        stage1(2, 0, 0, 3, 1)
-        stage1(1, 0, 1, 3, 3)
-        stage1(0, 0, 0, 3, 1)
-        stage1(0, 0, 0, 1, 0)
+        stage1(2, 0, 1, 0, 5)
         load_channel(3, 0)
-        group_channel(3, 0, "V", 256, 512)
-        group_channel(3, 0, "S", 0, 256)
+        stage1(2, 0, 1, 2, 7)
+        stage1(2, 0, 1, 3, 6)
         load_wide(3)
-        group_wide(3, 0, "V")
+        stage1(2, 0, 0, 2, 2)
+        stage1(2, 0, 0, 3, 4)
+        stage1(2, 0, 0, 0, 1)
+        group_channel(3, 0, "V", 256, 512)
+        stage1(1, 0, 0, 0, 1)
         load_wide(4)
-        quant_channel(3, 0)
-        stage1(0, 0, 0, 0, 7)
-        load_wide(5)
-        stage1(2, 0, 1, 0, 6)
-        quant_wide(3, 0)
-        stage1(3, 0, 0, 3, 1)
-        stage1(3, 0, 0, 2, 2)
-        stage1(3, 0, 0, 0, 7)
-        stage1(3, 0, 0, 1, 0)
-        group_wide(4, 1, "V")
+        stage1(1, 0, 0, 1, 3)
+        stage1(1, 0, 0, 3, 4)
+        stage1(2, 0, 0, 1, 3)
+        stage1(1, 0, 0, 2, 2)
+        stage1(2, 0, 1, 1, 0)
+        group_channel(3, 0, "S", 0, 256)
+        widen_weights()
+        group_wide(3, 0, "V")
         group_wide(3, 1, "S")
+        quant_channel(3, 0)
+        quant_wide(3, 0)
+        stage1(3, 0, 0, 0, 1)
         quant_wide(3, 1)
-        stage1(3, 0, 1, 2, 5)
-        stage1(3, 0, 1, 0, 6)
+        stage1(3, 0, 1, 2, 7)
+        stage1(3, 0, 1, 0, 5)
+        stage1(3, 0, 1, 3, 6)
+        stage1(3, 0, 1, 1, 0)
+        group_wide(4, 1, "V")
         load_codebook(0)
-        stage1(3, 0, 1, 1, 4)
+        stage1(3, 0, 0, 3, 4)
+        stage1(3, 0, 0, 2, 2)
         quant_wide(4, 1)
-        stage1(4, 0, 1, 2, 5)
-        stage1(4, 0, 1, 1, 4)
-        stage1(4, 0, 1, 0, 6)
-        load_codebook(1)
+        stage1(4, 0, 1, 3, 6)
+        stage1(4, 0, 1, 0, 5)
+        stage1(3, 0, 0, 1, 3)
+        stage1(4, 0, 1, 1, 0)
+        stage1(4, 0, 1, 2, 7)
         group_wide(4, 0, "S")
         quant_wide(4, 0)
-        stage1(4, 0, 0, 0, 7)
-        stage1(4, 0, 0, 1, 0)
-        stage1(3, 0, 1, 3, 3)
         stage1(4, 0, 0, 2, 2)
+        stage1(4, 0, 0, 3, 4)
+        stage1(4, 0, 0, 0, 1)
+        stage1(4, 0, 0, 1, 3)
+        load_wide(5)
+        group_wide(5, 1, "S")
         group_wide(5, 0, "V")
         quant_wide(5, 0)
-        stage1(4, 0, 0, 3, 1)
         load_channel(3, 1)
-        group_wide(5, 1, "S")
-        quant_wide(5, 1)
-        stage1(4, 0, 1, 3, 3)
-        group_channel(3, 1, "S", 256, 512)
-        stage1(5, 0, 0, 3, 1)
-        weigh(0, 0, 3, "S")
-        stage1(5, 0, 0, 0, 7)
-        stage1(5, 0, 0, 1, 0)
-        stage1(5, 0, 1, 2, 5)
-        stage1(5, 0, 1, 3, 3)
-        weigh(0, 0, 1, "S")
-        load_channel(1, 1)
-        stage1(5, 0, 1, 0, 6)
-        group_channel(3, 1, "V", 0, 256)
+        load_codebook(1)
+        stage1(5, 0, 0, 3, 4)
         stage1(5, 0, 0, 2, 2)
-        weigh(0, 1, 3, "S")
-        group_channel(1, 1, "V", 0, 256)
+        stage1(5, 0, 0, 0, 1)
+        stage1(5, 0, 0, 1, 3)
+        quant_wide(5, 1)
         load_channel(2, 1)
-        stage1(4, 1, 1, 3, 1)
-        weigh(0, 0, 0, "S")
-        stage1(5, 0, 1, 1, 4)
-        stage1(4, 1, 1, 1, 0)
-        quant_channel(3, 1)
-        stage1(4, 1, 1, 2, 3)
-        stage1(3, 1, 1, 2, 3)
-        stage1(3, 1, 1, 1, 0)
-        group_channel(2, 1, "S", 256, 512)
-        weigh(0, 0, 2, "S")
-        group_channel(1, 1, "V", 256, 512)
-        quant_channel(1, 1)
-        stage1(1, 1, 1, 0, 7)
-        stage1(3, 1, 1, 3, 1)
-        stage1(1, 1, 1, 2, 3)
         group_channel(2, 1, "V", 0, 256)
-        stage1(1, 1, 1, 1, 0)
-        stage1(3, 1, 1, 0, 7)
+        group_channel(2, 1, "V", 256, 512)
+        stage1(5, 0, 1, 0, 5)
+        stage1(5, 0, 1, 1, 0)
+        stage1(5, 0, 1, 2, 7)
+        group_channel(3, 1, "S", 256, 512)
+        weigh(0, 0, 3, "S")
+        group_channel(3, 1, "V", 0, 256)
+        stage1(5, 0, 1, 3, 6)
+        weigh(0, 0, 0, "S")
+        stage1(5, 1, 1, 2, 4)
+        weigh(0, 1, 2, "V")
+        stage1(4, 1, 1, 1, 1)
+        weigh(0, 1, 1, "S")
         quant_channel(2, 1)
-        load_channel(0, 1)
-        stage1(2, 1, 1, 1, 0)
-        stage1(2, 1, 1, 0, 7)
-        load_precoder(0)
-        stage1(2, 1, 1, 3, 1)
-        stage1(2, 1, 1, 2, 3)
-        stage1(4, 1, 1, 0, 7)
-        group_vw(0, 0, "V", 256, 512)
-        weigh(0, 1, 1, "V")
-        stage1(5, 1, 1, 1, 0)
-        weigh(0, 1, 2, "S")
-        stage1(5, 1, 1, 3, 1)
-        turn_precoder(0, 1, 0, 2)
+        stage1(5, 1, 1, 1, 1)
         weigh(0, 1, 0, "S")
-        group_vw(0, 1, "S", 0, 256)
-        group_vw(0, 0, "V", 0, 256)
+        stage1(5, 1, 1, 0, 0)
+        stage1(5, 1, 1, 3, 7)
+        stage1(4, 1, 1, 3, 7)
+        load_channel(1, 1)
+        stage1(2, 1, 1, 2, 4)
+        quant_channel(3, 1)
+        group_channel(1, 1, "V", 0, 256)
+        weigh(0, 1, 3, "S")
         group_vw(0, 1, "V", 256, 512)
-        quant_vw(0, 0)
+        load_channel(0, 1)
+        stage1(2, 1, 1, 3, 7)
+        stage1(3, 1, 1, 1, 1)
+        group_channel(1, 1, "S", 256, 512)
+        weigh(0, 0, 1, "S")
+        quant_channel(1, 1)
+        weigh(0, 0, 2, "S")
+        stage1(2, 1, 1, 0, 0)
+        load_precoder(0)
         group_channel(0, 1, "V", 0, 256)
-        group_precoder(0, 1, 0, "S")
-        turn_precoder(0, 0, 0, 5)
-        group_precoder(0, 0, 0, "S")
-        turn_precoder(0, 0, 1, 6)
-        turn_precoder(0, 1, 1, 4)
-        group_channel(0, 1, "V", 256, 512)
-        group_precoder(0, 1, 1, "S")
-        group_precoder(0, 0, 1, "S")
-        quant_vw(0, 1)
-        quant_channel(0, 1)
         load_precoder(1)
-        turn_precoder(1, 0, 0, 2)
-        turn_precoder(1, 1, 0, 5)
-        group_precoder(1, 1, 0, "S")
-        turn_precoder(1, 1, 1, 4)
-        group_precoder(1, 1, 1, "S")
-        quant_precoder(0, 1)
-        turn_precoder(1, 0, 1, 6)
-        stage1(0, 1, 1, 1, 0)
-        group_precoder(1, 0, 1, "S")
-        quant_precoder(0, 0)
-        group_precoder(1, 0, 0, "V")
-        weigh(1, 1, 1, "S")
-        quant_precoder(1, 1)
-        load_extra(1, 1)
-        stage1(0, 1, 1, 3, 1)
-        stage1(1, 1, 1, 3, 1)
-        weigh(1, 1, 3, "S")
-        load_extra(0, 0)
-        stage2(2, 0, 5)
-        stage2(3, 0, 4)
-        stage1(0, 1, 0, 1, 2)
-        quant_precoder(1, 0)
-        stage2(3, 1, 6)
-        add_extra(2, 0)
-        add_extra(3, 0)
-        finish_y(3, 0)
-        load_extra(0, 1)
-        round_y(3, 0, "S")
-        store_y(3, 0)
-        stage2(2, 1, 0)
-        add_extra(2, 1)
-        stage1(5, 1, 1, 2, 3)
-        finish_y(2, 0)
-        round_y(2, 0, "S")
-        stage2(0, 0, 1)
-        stage1(5, 1, 1, 0, 7)
-        stage1(0, 1, 1, 0, 7)
-        weigh(1, 1, 0, "S")
-        stage2(1, 1, 5)
         load_extra(1, 0)
-        stage1(0, 1, 1, 2, 3)
-        weigh(1, 1, 2, "S")
-        stage1(0, 1, 0, 3, 4)
-        group_vw(1, 1, "S", 256, 512)
-        stage1(4, 1, 0, 2, 0)
-        add_extra(3, 1)
-        finish_y(3, 1)
-        store_y(3, 1)
-        add_extra(1, 1)
-        finish_y(2, 1)
-        store_y(2, 0)
-        finish_y(1, 1)
-        stage2(0, 1, 6)
-        stage1(4, 1, 0, 3, 4)
-        add_extra(0, 1)
-        round_y(1, 1, "S")
-        stage1(0, 1, 0, 0, 7)
-        round_y(2, 1, "S")
-        stage1(4, 1, 0, 0, 7)
-        add_extra(0, 0)
-        finish_y(0, 0)
-        stage1(4, 1, 0, 1, 2)
-        stage1(1, 1, 0, 3, 4)
-        store_y(2, 1)
+        group_vw(0, 0, "V", 0, 256)
+        stage1(3, 1, 1, 0, 0)
+        stage1(3, 1, 1, 3, 7)
+        stage1(3, 1, 1, 2, 4)
+        turn_precoder(0, 1, 1, 5)
+        group_precoder(0, 1, 1, "S")
+        turn_precoder(0, 1, 0, 6)
+        gains_turn(3)
+        gains_cols()
+        group_vw(0, 1, "V", 0, 256)
+        turn_precoder(0, 0, 0, 2)
+        group_precoder(0, 1, 0, "S")
+        group_precoder(0, 0, 0, "S")
+        group_channel(0, 1, "V", 256, 512)
+        quant_vw(0, 1)
+        turn_precoder(0, 0, 1, 5)
+        turn_precoder(1, 1, 0, 3)
+        quant_precoder(0, 1)
+        group_precoder(0, 0, 1, "S")
+        quant_precoder(0, 0)
+        group_vw(0, 0, "S", 256, 512)
+        turn_precoder(1, 0, 1, 6)
+        turn_precoder(1, 1, 1, 2)
+        turn_precoder(1, 0, 0, 5)
+        stage1(4, 1, 1, 0, 0)
+        stage1(1, 1, 1, 0, 0)
+        quant_vw(0, 0)
+        group_precoder(1, 0, 1, "S")
+        stage1(1, 1, 1, 1, 1)
+        group_precoder(1, 0, 0, "S")
+        quant_channel(0, 1)
+        stage2(2, 0, 6)
+        stage2(3, 0, 5)
+        quant_precoder(1, 0)
+        group_precoder(1, 1, 0, "S")
+        stage1(0, 1, 1, 0, 0)
+        load_extra(0, 0)
+        add_extra(2, 0)
         stage2(1, 0, 3)
+        add_extra(3, 0)
+        stage2(0, 0, 6)
+        finish_y(2, 0)
+        stage1(4, 1, 1, 2, 4)
+        stage1(1, 1, 1, 2, 4)
+        group_precoder(1, 1, 1, "S")
+        stage1(0, 1, 1, 2, 4)
+        quant_precoder(1, 1)
+        load_extra(0, 1)
+        finish_y(3, 0)
         add_extra(1, 0)
-        stage1(2, 1, 0, 3, 4)
-        finish_y(0, 1)
-        turn_y(2, 2, 0, 5)
-        group_y(2, 2, 0, "S")
-        quant_y(2, 2, 0)
-        stage1(2, 1, 0, 0, 7)
-        store_codes(2, 2, 0)
+        stage1(2, 1, 1, 1, 1)
+        add_extra(0, 0)
         finish_y(1, 0)
-        round_y(0, 1, "V")
-        stage1(3, 1, 0, 0, 7)
-        round_y(0, 0, "S")
-        stage1(5, 1, 0, 1, 2)
-        stage1(1, 1, 0, 0, 7)
-        stage1(1, 1, 0, 1, 2)
-        stage1(2, 1, 0, 1, 2)
-        stage1(5, 1, 0, 3, 4)
-        store_y(0, 1)
-        store_y(1, 1)
-        stage1(5, 1, 0, 0, 7)
+        stage2(3, 1, 2)
+        add_extra(3, 1)
+        load_extra(1, 1)
+        round_y(2, 0, "S")
+        round_y(3, 0, "S")
+        weigh(1, 1, 2, "S")
+        stage1(0, 1, 1, 1, 1)
+        stage2(1, 1, 5)
+        weigh(1, 1, 0, "S")
+        store_y(2, 0)
+        weigh(1, 1, 1, "S")
+        turn_y(2, 2, 0, 3)
+        finish_y(3, 1)
+        group_y(2, 2, 0, "S")
+        round_y(1, 0, "S")
+        stage1(1, 1, 1, 3, 7)
+        stage1(0, 1, 1, 3, 7)
+        stage2(0, 1, 6)
+        weigh(1, 1, 3, "S")
         group_vw(1, 1, "S", 0, 256)
-        quant_vw(1, 1)
-        stage1(1, 1, 0, 2, 0)
-        weigh(1, 0, 0, "S")
-        store_y(1, 0)
-        stage1(3, 1, 0, 1, 2)
-        weigh(1, 0, 1, "V")
-        round_y(3, 1, "V")
-        stage1(3, 1, 0, 3, 4)
+        stage1(1, 1, 0, 1, 4)
+        add_extra(1, 1)
+        finish_y(1, 1)
+        store_y(3, 0)
+        quant_y(2, 2, 0)
+        stage1(5, 1, 0, 1, 4)
+        store_y(1, 1)
+        stage1(2, 1, 0, 3, 0)
+        finish_y(0, 0)
+        store_y(0, 0)
+        stage1(3, 1, 0, 0, 2)
+        add_extra(0, 1)
+        finish_y(0, 1)
+        stage2(2, 1, 1)
+        add_extra(2, 1)
+        stage1(5, 1, 0, 3, 0)
+        finish_y(2, 1)
+        stage1(4, 1, 0, 3, 0)
+        round_y(1, 1, "S")
+        stage1(4, 1, 0, 0, 2)
+        stage1(0, 1, 0, 1, 4)
+        stage1(3, 1, 0, 1, 4)
+        round_y(3, 1, "S")
+        group_vw(1, 1, "V", 256, 512)
+        stage1(0, 1, 0, 0, 2)
+        stage1(3, 1, 0, 3, 0)
+        stage1(0, 1, 0, 3, 0)
+        store_y(0, 1)
+        round_y(2, 1, "V")
+        stage1(1, 1, 0, 3, 0)
+        round_y(0, 0, "S")
+        stage1(1, 1, 0, 0, 2)
         weigh(1, 0, 3, "S")
-        stage1(0, 1, 0, 2, 0)
-        stage1(2, 1, 0, 2, 0)
-        stage1(5, 1, 0, 2, 0)
-        stage1(3, 1, 0, 2, 0)
-        weigh(1, 0, 2, "V")
-        turn_y(0, 2, 1, 6)
-        group_vw(1, 0, "S", 0, 256)
+        stage1(2, 1, 0, 0, 2)
+        stage1(0, 1, 0, 2, 3)
+        store_codes(2, 2, 0)
+        quant_vw(1, 1)
+        stage1(5, 1, 0, 2, 3)
+        stage1(3, 1, 0, 2, 3)
+        stage1(4, 1, 0, 2, 3)
+        stage1(2, 1, 0, 2, 3)
+        stage1(1, 1, 0, 2, 3)
+        weigh(1, 0, 2, "S")
+        stage1(5, 1, 0, 0, 2)
+        stage1(4, 1, 0, 1, 4)
+        stage1(2, 1, 0, 1, 4)
+        weigh(1, 0, 1, "S")
+        weigh(1, 0, 0, "V")
+        turn_y(0, 2, 0, 5)
+        round_y(0, 1, "V")
+        group_y(0, 2, 0, "S")
+        store_y(2, 1)
+        store_y(3, 1)
+        turn_y(0, 2, 1, 7)
         group_y(0, 2, 1, "S")
+        group_vw(1, 0, "V", 0, 256)
+        turn_y(2, 2, 1, 6)
         group_vw(1, 0, "V", 256, 512)
         quant_vw(1, 0)
-        turn_y(2, 2, 1, 1)
-        stage2(7, 0, 5)
-        stage2(6, 0, 3)
+        store_y(1, 0)
+        stage2(7, 0, 1)
+        quant_y(0, 2, 0)
         quant_y(0, 2, 1)
         group_y(2, 2, 1, "S")
         quant_y(2, 2, 1)
-        store_y(0, 0)
+        store_codes(2, 2, 1)
+        stage2(6, 0, 0)
+        store_scales(0, [nc.sync] * 4)
+        store_codes(0, 2, 0)
         add_extra(7, 0)
+        stage2(6, 1, 3)
         add_extra(6, 0)
         finish_y(7, 0)
         store_y(7, 0)
-        store_codes(2, 2, 1)
-        round_y(1, 0, "S")
-        finish_y(6, 0)
-        store_y(6, 0)
-        turn_y(0, 2, 0, 7)
-        group_y(0, 2, 0, "S")
-        stage2(4, 0, 4)
-        add_extra(4, 0)
+        round_y(7, 0, "S")
         stage2(4, 1, 2)
         add_extra(4, 1)
-        finish_y(4, 0)
-        quant_y(0, 2, 0)
-        stage2(5, 1, 0)
-        add_extra(5, 1)
-        finish_y(4, 1)
-        stage2(5, 0, 6)
-        finish_y(5, 1)
-        store_codes(0, 2, 1)
-        store_y(4, 1)
-        store_codes(0, 2, 0)
-        stage2(6, 1, 1)
+        finish_y(6, 0)
         round_y(6, 0, "S")
-        store_y(5, 1)
-        round_y(7, 0, "S")
-        store_y(4, 0)
-        add_extra(6, 1)
-        round_y(4, 0, "S")
-        turn_y(6, 2, 0, 5)
+        finish_y(4, 1)
+        round_y(4, 1, "S")
+        stage2(5, 1, 4)
+        add_extra(5, 1)
+        stage2(4, 0, 5)
+        add_extra(4, 0)
+        finish_y(5, 1)
+        finish_y(4, 0)
+        store_y(6, 0)
+        turn_y(6, 2, 0, 7)
+        group_y(6, 2, 0, "S")
+        stage2(5, 0, 6)
+        round_y(5, 1, "S")
+        store_y(4, 1)
+        turn_y(4, 2, 1, 1)
         add_extra(5, 0)
-        store_scales(0, [nc.sync] * 4)
+        store_codes(0, 2, 1)
+        round_y(4, 0, "S")
+        add_extra(6, 1)
+        finish_y(5, 0)
+        round_y(5, 0, "S")
+        store_y(4, 0)
+        store_y(5, 1)
         finish_y(6, 1)
         store_y(6, 1)
-        round_y(4, 1, "S")
-        stage2(7, 1, 3)
-        round_y(5, 1, "S")
-        group_y(6, 2, 0, "S")
-        finish_y(5, 0)
-        store_y(5, 0)
+        stage2(7, 1, 0)
         add_extra(7, 1)
-        quant_y(6, 2, 0)
-        store_codes(6, 2, 0)
+        turn_y(4, 2, 0, 2)
         round_y(6, 1, "S")
-        turn_y(4, 2, 1, 7)
+        turn_y(6, 1, 1, 4)
+        quant_y(6, 2, 0)
         finish_y(7, 1)
-        store_y(7, 1)
-        round_y(5, 0, "S")
-        turn_y(4, 2, 0, 4)
-        group_y(4, 2, 1, "S")
-        turn_y(6, 1, 1, 2)
-        group_y(6, 1, 1, "S")
         round_y(7, 1, "V")
-        turn_y(7, 1, 1, 0)
-        quant_y(6, 1, 1)
-        quant_y(4, 2, 1)
         group_y(4, 2, 0, "S")
+        group_y(4, 2, 1, "S")
+        store_y(5, 0)
+        group_y(6, 1, 1, "S")
+        store_codes(6, 2, 0)
         quant_y(4, 2, 0)
         store_codes(4, 2, 0)
-        group_y(7, 1, 1, "S")
-        quant_y(7, 1, 1)
+        quant_y(4, 2, 1)
         store_codes(4, 2, 1)
+        quant_y(6, 1, 1)
+        turn_y(7, 1, 1, 5)
+        group_y(7, 1, 1, "S")
+        store_y(7, 1)
+        quant_y(7, 1, 1)
         store_scales(1, [nc.sync] * 4)
         store_codes(6, 2, 1)

@@ -20,17 +20,16 @@ ADD = mybir.AluOpType.add
 P = 128
 HALF = 512
 PASSES = [("h", 0), ("h", 1), ("h", 2), ("h", 3), ("c", 0), ("c", 1)]
-GROUPED_BUFS = 7
+GROUPED_BUFS = {1: 3, 2: 3}
 WIDE_BUFS = 4
-NARROW_BUFS = 6
-VW_BUFS = 2
-Y_BUFS = 6
-SUM_BUFS = 4
-RND_BUFS = 5
-GY_BUFS = 4
+NARROW_BUFS = 5
+VW_BUFS = 3
+Y_BUFS = 3
+SUM_BUFS = 2
+RND_BUFS = 3
+GY_BUFS = 2
 WIDE_OUT = "p (t m j) -> p m j t"
 WIDE_IN = "p j (m t) -> p m j t"
-WB1 = "SSSS"
 
 
 def tile_weighted_transmit_covariance_block_k6_kernel(
@@ -53,8 +52,17 @@ def tile_weighted_transmit_covariance_block_k6_kernel(
             scales = keep.tile([P, width], U8, name=name + "_scales", align_bytes=64)
             return codes, scales
 
-        def grouped_tile(name):
-            return stage.tile([P, 4 * HALF], BF16, name=name, tag="grouped", bufs=GROUPED_BUFS, align_bytes=64)
+        def grouped_tile(key, parts):
+            if key not in T:
+                name = "_".join(str(x) for x in key)
+                T[key] = stage.tile([P, parts, 4 * HALF], BF16, name=name, tag="grouped%d" % parts, bufs=GROUPED_BUFS[parts], align_bytes=64)
+            return T[key]
+
+        def quantise_parts(kind, key, first, count, parts):
+            if ("q" + kind,) + key not in T:
+                T[("q" + kind,) + key] = quantised("q" + kind + "_".join(str(x) for x in key), HALF * parts)
+            source = T[("g" + kind,) + key][:, first : first + count, :].rearrange("p a c -> p (a c)")
+            quantise(T[("q" + kind,) + key], slice(HALF * first, HALF * (first + count)), source)
 
         def copy_on(engine, out, in_):
             if engine == "V":
@@ -66,19 +74,25 @@ def tile_weighted_transmit_covariance_block_k6_kernel(
             codes, scales = pair
             nc.vector.quantize_mx(out=codes[:, cols].bitcast(FP8X4), scales=scales[:, cols], in_=source)
 
-        def load_wide(s):
+        def load_wide(s, g):
             kind, k = PASSES[s]
             src = coef if kind == "h" else beam_coef
-            raw = stage.tile([P, 4, U], BF16, name="wide%d" % s, tag="wide", bufs=WIDE_BUFS)
-            nc.sync.dma_start(out=raw[:], in_=src[HALF * k : HALF * (k + 1), :].rearrange("(p j) u -> p j u", j=4))
-            T["wide", s] = raw
+            raw = stage.tile([P, 4, HALF], BF16, name="wide%d_%d" % (s, g), tag="narrow", bufs=NARROW_BUFS)
+            rows = src[HALF * k : HALF * (k + 1), HALF * g : HALF * (g + 1)]
+            nc.sync.dma_start(out=raw[:], in_=rows.rearrange("(p j) u -> p j u", j=4))
+            T["wide", s, g] = raw
 
-        def load_channel(s, mh):
-            k = PASSES[s][1]
+        def load_channel(s):
+            raw = stage.tile([P, 4, M], BF16, name="chan%d" % s, tag="wide", bufs=WIDE_BUFS)
+            nc.sync.dma_start(out=raw[:], in_=channel[HALF * s : HALF * (s + 1), :].rearrange("(p j) m -> p j m", j=4))
+            for mh in range(2):
+                T["chan", s, mh] = raw[:, :, HALF * mh : HALF * (mh + 1)]
+
+        def load_channel_half(s, mh):
             raw = stage.tile([P, 4, HALF], BF16, name="chan%d_%d" % (s, mh), tag="narrow", bufs=NARROW_BUFS)
-            rows = channel[HALF * k : HALF * (k + 1), HALF * mh : HALF * (mh + 1)]
+            rows = channel[HALF * s : HALF * (s + 1), HALF * mh : HALF * (mh + 1)]
             nc.sync.dma_start(out=raw[:], in_=rows.rearrange("(p j) m -> p j m", j=4))
-            T["chan", s, mh] = raw
+            T["chan", s, mh] = raw[:]
 
         def load_codebook(k):
             nc.sync.dma_start(out=book_words[:, k, :].bitcast(I32), in_=codebook_words[k].bitcast(I32))
@@ -88,24 +102,20 @@ def tile_weighted_transmit_covariance_block_k6_kernel(
             nc.sync.dma_start(out=raw[:], in_=precoder2[HALF * nh : HALF * (nh + 1), :].rearrange("(j p) u -> p j u", p=P))
             T["prec", nh] = raw
 
-        def load_extra(mh, nh):
-            raw = stage.tile([P, 4, HALF], BF16, name="extra%d_%d" % (mh, nh), tag="narrow", bufs=NARROW_BUFS)
-            rows = extra[HALF * mh : HALF * (mh + 1), HALF * nh : HALF * (nh + 1)]
-            nc.sync.dma_start(out=raw[:], in_=rows.rearrange("(j p) n -> p j n", p=P))
-            T["extra", mh, nh] = raw
+        def load_extra(mh):
+            raw = stage.tile([P, 4, N], BF16, name="extra%d" % mh, tag="wide", bufs=WIDE_BUFS)
+            nc.sync.dma_start(out=raw[:], in_=extra[HALF * mh : HALF * (mh + 1), :].rearrange("(j p) n -> p j n", p=P))
+            T["extra", mh] = raw
 
         def group_wide(s, g, engine):
-            grouped = grouped_tile("gw%d_%d" % (s, g))
             copy_on(
                 engine,
-                grouped[:].rearrange(WIDE_OUT, t=4, j=4),
-                T["wide", s][:, :, HALF * g : HALF * (g + 1)].rearrange(WIDE_IN, t=4),
+                grouped_tile(("gw", s, g), 1)[:, 0, :].rearrange(WIDE_OUT, t=4, j=4),
+                T["wide", s, g][:].rearrange(WIDE_IN, t=4),
             )
-            T["gw", s, g] = grouped
 
         def quant_wide(s, g):
-            T["qw", s, g] = quantised("qw%d_%d" % (s, g), HALF)
-            quantise(T["qw", s, g], slice(0, HALF), T["gw", s, g][:])
+            quantise_parts("w", (s, g), 0, 1, 1)
 
         def interleave(engine, grouped, rows, lo, hi):
             copy_on(
@@ -115,13 +125,10 @@ def tile_weighted_transmit_covariance_block_k6_kernel(
             )
 
         def group_channel(s, mh, engine, lo, hi):
-            if ("gc", s, mh) not in T:
-                T["gc", s, mh] = grouped_tile("gc%d_%d" % (s, mh))
-            interleave(engine, T["gc", s, mh], T["chan", s, mh], lo, hi)
+            interleave(engine, grouped_tile(("gc", s), 2)[:, mh, :], T["chan", s, mh], lo, hi)
 
-        def quant_channel(s, mh):
-            T["qc", s, mh] = quantised("qc%d_%d" % (s, mh), HALF)
-            quantise(T["qc", s, mh], slice(0, HALF), T["gc", s, mh][:])
+        def quant_channel(s, first, count):
+            quantise_parts("c", (s,), first, count, 2)
 
         def stage1(s, mh, g, t, b):
             kind, k = PASSES[s]
@@ -132,8 +139,8 @@ def tile_weighted_transmit_covariance_block_k6_kernel(
             codes, scales = T["qw", s, g]
             cols = slice(P * t, P * (t + 1))
             if kind == "h":
-                rhs = T["qc", s, mh][0][:].bitcast(FP8X4)
-                rhs_scale = T["qc", s, mh][1][:]
+                rhs = T["qc", s][0][:, HALF * mh : HALF * (mh + 1)].bitcast(FP8X4)
+                rhs_scale = T["qc", s][1][:, HALF * mh : HALF * (mh + 1)]
             else:
                 rhs = book_words[:, k, 2 * HALF * mh : 2 * HALF * (mh + 1)].bitcast(FP4X4)
                 rhs_scale = book_scales[:, k, HALF * mh : HALF * (mh + 1)]
@@ -153,13 +160,10 @@ def tile_weighted_transmit_covariance_block_k6_kernel(
                 nc.scalar.activation(out=out, in_=T["acc1", mh, g, t][:], func=COPY, scale=weight)
 
         def group_vw(mh, g, engine, lo, hi):
-            if ("gv", mh, g) not in T:
-                T["gv", mh, g] = grouped_tile("gv%d_%d" % (mh, g))
-            interleave(engine, T["gv", mh, g], T["vw", mh, g], lo, hi)
+            interleave(engine, grouped_tile(("gv", mh), 2)[:, g, :], T["vw", mh, g][:], lo, hi)
 
-        def quant_vw(mh, g):
-            T["qv", mh, g] = quantised("qv%d_%d" % (mh, g), HALF)
-            quantise(T["qv", mh, g], slice(0, HALF), T["gv", mh, g][:])
+        def quant_vw(mh, first, count):
+            quantise_parts("v", (mh,), first, count, 2)
 
         def turn_precoder(nh, g, jj, b):
             words = T["prec", nh][:].bitcast(F32)
@@ -170,65 +174,70 @@ def tile_weighted_transmit_covariance_block_k6_kernel(
             T["pt", nh, g, jj] = turned
 
         def group_precoder(nh, g, jj, engine):
-            if ("gp", nh, g) not in T:
-                T["gp", nh, g] = grouped_tile("gp%d_%d" % (nh, g))
-            out = T["gp", nh, g][:].bitcast(F32)[:, HALF * jj : HALF * (jj + 1)].rearrange("p (j r h) -> p j r h", j=2, h=2)
+            words = grouped_tile(("gp", nh), 2)[:, g, :].bitcast(F32)
+            out = words[:, HALF * jj : HALF * (jj + 1)].rearrange("p (j r h) -> p j r h", j=2, h=2)
             copy_on(engine, out, T["pt", nh, g, jj][:].rearrange("p j h r -> p j r h"))
 
-        def quant_precoder(nh, g):
-            T["qp", nh, g] = quantised("qp%d_%d" % (nh, g), HALF)
-            quantise(T["qp", nh, g], slice(0, HALF), T["gp", nh, g][:])
+        def quant_precoder(nh):
+            quantise_parts("p", (nh,), 0, 2, 2)
 
         def stage2(mt, nh, b):
             acc = bank(b, [P, HALF], F32, "acc2_%d_%d" % (mt, nh))
-            cols = slice(P * (mt % 4), P * (mt % 4 + 1))
+            codes, scales = T["qv", mt // 4]
             for g in range(2):
-                codes, scales = T["qv", mt // 4, g]
+                cols = slice(HALF * g + P * (mt % 4), HALF * g + P * (mt % 4 + 1))
+                moving = slice(HALF * g, HALF * (g + 1))
                 nc.tensor.matmul_mx(
                     out=acc[:], lhsT=codes[:, cols].bitcast(FP8X4), lhsT_scale=scales[:, cols],
-                    rhs=T["qp", nh, g][0][:].bitcast(FP8X4), rhs_scale=T["qp", nh, g][1][:],
+                    rhs=T["qp", nh][0][:, moving].bitcast(FP8X4), rhs_scale=T["qp", nh][1][:, moving],
                     start=(g == 0), stop=(g == 1),
                 )
             T["acc2", mt, nh] = acc
 
         def add_extra(mt, nh):
-            summed = stage.tile([P, HALF], F32, name="sum%d_%d" % (mt, nh), tag="summed", bufs=SUM_BUFS)
+            if ("sum", mt) not in T:
+                T["sum", mt] = stage.tile([P, N], F32, name="sum%d" % mt, tag="summed", bufs=SUM_BUFS)
+            cols = slice(HALF * nh, HALF * (nh + 1))
             nc.vector.scalar_tensor_tensor(
-                out=summed[:], in0=T["acc2", mt, nh][:], scalar=gain1_cols[:, mt : mt + 1],
-                in1=T["extra", mt // 4, nh][:, mt % 4, :], op0=MULT, op1=ADD,
+                out=T["sum", mt][:, cols], in0=T["acc2", mt, nh][:], scalar=gain1_cols[:, mt : mt + 1],
+                in1=T["extra", mt // 4][:, mt % 4, cols], op0=MULT, op1=ADD,
             )
-            T["sum", mt, nh] = summed
 
-        def finish_y(mt, nh):
-            y = stage.tile([P, HALF], F32, name="y%d_%d" % (mt, nh), tag="y", bufs=Y_BUFS)
-            nc.vector.tensor_tensor(out=y[:], in0=T["sum", mt, nh][:], in1=gain2_rows[:, HALF * nh : HALF * (nh + 1)], op=MULT)
-            T["y", mt, nh] = y
+        def finish_y(mt, first, count, engine):
+            if ("y", mt) not in T:
+                T["y", mt] = stage.tile([P, N], F32, name="y%d" % mt, tag="y", bufs=Y_BUFS)
+            cols = slice(HALF * first, HALF * (first + count))
+            (nc.vector if engine == "V" else nc.gpsimd).tensor_tensor(out=T["y", mt][:, cols], in0=T["sum", mt][:, cols], in1=gain2_rows[:, cols], op=MULT)
 
-        def store_y(mt, nh):
-            nc.sync.dma_start(out=out_0[P * mt : P * (mt + 1), HALF * nh : HALF * (nh + 1)], in_=T["y", mt, nh][:])
+        def store_y(mt, first, count):
+            cols = slice(HALF * first, HALF * (first + count))
+            nc.sync.dma_start(out=out_0[P * mt : P * (mt + 1), cols], in_=T["y", mt][:, cols])
 
         def round_y(mt, nh, engine):
-            rounded = stage.tile([P, HALF], BF16, name="yb%d_%d" % (mt, nh), tag="rounded", bufs=RND_BUFS)
-            copy_on(engine, rounded[:].rearrange("m (h p e) -> m h p e", h=2, e=2), T["y", mt, nh][:].rearrange("m (p h e) -> m h p e", h=2, e=2))
-            T["yb", mt, nh] = rounded
+            if ("yb", mt) not in T:
+                T["yb", mt] = stage.tile([P, N], BF16, name="yb%d" % mt, tag="rounded", bufs=RND_BUFS)
+            cols = slice(HALF * nh, HALF * (nh + 1))
+            copy_on(engine, T["yb", mt][:, cols].rearrange("m (h p e) -> m h p e", h=2, e=2), T["y", mt][:, cols].rearrange("m (p h e) -> m h p e", h=2, e=2))
 
-        def turn_y(mt0, count, nh, b):
-            turned = bank(b, [P, count, 2, P], F32, "yt%d_%d" % (mt0, nh))
+        def turn_y(mt, first, count, b):
+            turned = bank(b, [P, count, 2, P], F32, "yt%d_%d" % (mt, first))
+            words = T["yb", mt][:].bitcast(F32)
             for i in range(count):
-                words = T["yb", mt0 + i, nh][:].bitcast(F32)
                 for h in range(2):
-                    nc.tensor.transpose(turned[:, i, h, :], words[:, P * h : P * (h + 1)], ident_f32[:])
-            T["yt", mt0, nh] = turned
+                    at = 2 * P * (first + i) + P * h
+                    nc.tensor.transpose(turned[:, i, h, :], words[:, at : at + P], ident_f32[:])
+            T["yt", mt, first] = turned
 
-        def group_y(mt0, count, nh, engine):
-            grouped = stage.tile([P, 4 * P * count], BF16, name="gy%d_%d" % (mt0, nh), tag="grouped_y", bufs=GY_BUFS, align_bytes=64)
-            copy_on(engine, grouped[:].bitcast(F32).rearrange("p (i m h) -> p i m h", i=count, h=2), T["yt", mt0, nh][:].rearrange("p i h m -> p i m h"))
-            T["gy", mt0, nh] = grouped
+        def group_y(mt, first, count, engine):
+            if ("gy", mt // 2) not in T:
+                T["gy", mt // 2] = stage.tile([P, 2, 2, 4 * P], BF16, name="gy%d" % (mt // 2), tag="grouped_y", bufs=GY_BUFS, align_bytes=64)
+            out = T["gy", mt // 2][:, first : first + count, mt % 2, :].bitcast(F32).rearrange("p g (m h) -> p g m h", h=2)
+            copy_on(engine, out, T["yt", mt, first][:].rearrange("p g h m -> p g m h"))
 
         def quant_y(mt0, count, nh):
             cols = slice(P * (mt0 % 4), P * (mt0 % 4 + count))
             codes, scales = y_planes[mt0 // 4]
-            nc.vector.quantize_mx(out=codes[:, nh, cols].bitcast(FP8X4), scales=scales[:, nh, cols], in_=T["gy", mt0, nh][:])
+            nc.vector.quantize_mx(out=codes[:, nh, cols].bitcast(FP8X4), scales=scales[:, nh, cols], in_=T["gy", mt0 // 2][:, nh, mt0 % 2 : mt0 % 2 + count, :].rearrange("p i c -> p (i c)"))
 
         def store_codes(mt0, count, nh):
             words = out_1[nh].rearrange("p m t -> p (m t)").bitcast(I32)
@@ -286,342 +295,318 @@ def tile_weighted_transmit_covariance_block_k6_kernel(
             for j in range(8):
                 nc.tensor.transpose(T["spread"][:, P * j : P * (j + 1)], gain2_cols[:, j : j + 1].to_broadcast([P, P]), ident_bf16[:])
 
-        def gains_rows():
-            nc.scalar.copy(out=gain2_rows[:].rearrange("q (p j) -> q p j", j=8), in_=T["spread"][:].rearrange("q (j p) -> q p j", j=8))
+        def gains_rows(engine):
+            copy_on(engine, gain2_rows[:].rearrange("q (p j) -> q p j", j=8), T["spread"][:].rearrange("q (j p) -> q p j", j=8))
 
-        load_channel(0, 0)
-        group_channel(0, 0, "V", 0, 256)
-        group_channel(0, 0, "V", 256, 512)
-        load_wide(0)
-        quant_channel(0, 0)
+        load_channel(1)
         gains_spread(0)
-        gains_rows()
+        gains_rows("V")
+        group_channel(1, 1, "V", 0, 512)
+        load_wide(1, 0)
+        group_wide(1, 0, "V")
+        group_channel(1, 0, "S", 256, 512)
+        quant_wide(1, 0)
+        group_channel(1, 0, "S", 0, 256)
+        quant_channel(1, 0, 2)
+        stage1(1, 1, 0, 1, 1)
+        stage1(1, 0, 0, 1, 2)
+        stage1(1, 1, 0, 3, 3)
+        load_channel_half(0, 0)
+        load_channel_half(0, 1)
+        stage1(1, 0, 0, 0, 4)
+        group_channel(0, 0, "S", 0, 256)
+        group_channel(0, 0, "S", 256, 512)
+        group_channel(0, 1, "S", 0, 512)
+        quant_channel(0, 0, 1)
+        stage1(1, 1, 0, 2, 5)
+        load_wide(0, 0)
         group_wide(0, 0, "V")
         quant_wide(0, 0)
-        stage1(0, 0, 0, 0, 1)
-        stage1(0, 0, 0, 2, 2)
-        stage1(0, 0, 0, 1, 3)
-        stage1(0, 0, 0, 3, 4)
-        load_wide(1)
-        group_wide(1, 0, "V")
-        quant_wide(1, 0)
-        load_channel(1, 0)
-        group_wide(0, 1, "S")
-        quant_wide(0, 1)
-        stage1(0, 0, 1, 0, 5)
-        stage1(0, 0, 1, 3, 6)
-        group_wide(1, 1, "S")
-        quant_wide(1, 1)
-        stage1(0, 0, 1, 2, 7)
-        group_channel(1, 0, "V", 0, 256)
-        group_channel(1, 0, "S", 256, 512)
-        quant_channel(1, 0)
-        stage1(1, 0, 1, 0, 5)
-        stage1(1, 0, 1, 3, 6)
-        stage1(1, 0, 1, 1, 0)
-        load_wide(2)
-        group_wide(2, 1, "S")
-        group_wide(2, 0, "V")
-        load_channel(2, 0)
-        stage1(0, 0, 1, 1, 0)
-        group_channel(2, 0, "V", 0, 256)
-        group_channel(2, 0, "S", 256, 512)
-        quant_wide(2, 1)
-        quant_wide(2, 0)
-        stage1(1, 0, 1, 2, 7)
-        quant_channel(2, 0)
-        stage1(2, 0, 1, 0, 5)
-        load_channel(3, 0)
-        stage1(2, 0, 1, 2, 7)
-        stage1(2, 0, 1, 3, 6)
-        load_wide(3)
-        stage1(2, 0, 0, 2, 2)
-        stage1(2, 0, 0, 3, 4)
-        stage1(2, 0, 0, 0, 1)
-        group_channel(3, 0, "V", 256, 512)
-        stage1(1, 0, 0, 0, 1)
-        load_wide(4)
-        stage1(1, 0, 0, 1, 3)
-        stage1(1, 0, 0, 3, 4)
-        stage1(2, 0, 0, 1, 3)
-        stage1(1, 0, 0, 2, 2)
-        stage1(2, 0, 1, 1, 0)
-        group_channel(3, 0, "S", 0, 256)
+        stage1(0, 0, 0, 1, 2)
+        stage1(0, 0, 0, 0, 4)
+        stage1(1, 0, 0, 3, 6)
+        stage1(0, 0, 0, 3, 6)
+        quant_channel(0, 1, 1)
+        stage1(0, 1, 0, 0, 7)
+        load_wide(5, 0)
+        load_channel(2)
+        stage1(0, 1, 0, 1, 1)
+        stage1(0, 0, 0, 2, 0)
+        load_wide(2, 0)
+        stage1(0, 1, 0, 3, 3)
+        group_wide(5, 0, "S")
+        stage1(0, 1, 0, 2, 5)
         widen_weights()
-        group_wide(3, 0, "V")
-        group_wide(3, 1, "S")
-        quant_channel(3, 0)
-        quant_wide(3, 0)
-        stage1(3, 0, 0, 0, 1)
-        quant_wide(3, 1)
-        stage1(3, 0, 1, 2, 7)
-        stage1(3, 0, 1, 0, 5)
-        stage1(3, 0, 1, 3, 6)
-        stage1(3, 0, 1, 1, 0)
-        group_wide(4, 1, "V")
-        load_codebook(0)
-        stage1(3, 0, 0, 3, 4)
-        stage1(3, 0, 0, 2, 2)
-        quant_wide(4, 1)
-        stage1(4, 0, 1, 3, 6)
-        stage1(4, 0, 1, 0, 5)
-        stage1(3, 0, 0, 1, 3)
-        stage1(4, 0, 1, 1, 0)
-        stage1(4, 0, 1, 2, 7)
-        group_wide(4, 0, "S")
-        quant_wide(4, 0)
-        stage1(4, 0, 0, 2, 2)
-        stage1(4, 0, 0, 3, 4)
-        stage1(4, 0, 0, 0, 1)
-        stage1(4, 0, 0, 1, 3)
-        load_wide(5)
-        group_wide(5, 1, "S")
-        group_wide(5, 0, "V")
+        group_channel(2, 0, "V", 0, 256)
         quant_wide(5, 0)
-        load_channel(3, 1)
+        stage1(1, 1, 0, 0, 7)
+        stage1(1, 0, 0, 2, 0)
+        group_channel(2, 1, "V", 0, 512)
         load_codebook(1)
-        stage1(5, 0, 0, 3, 4)
-        stage1(5, 0, 0, 2, 2)
-        stage1(5, 0, 0, 0, 1)
-        stage1(5, 0, 0, 1, 3)
-        quant_wide(5, 1)
-        load_channel(2, 1)
-        group_channel(2, 1, "V", 0, 256)
-        group_channel(2, 1, "V", 256, 512)
-        stage1(5, 0, 1, 0, 5)
-        stage1(5, 0, 1, 1, 0)
-        stage1(5, 0, 1, 2, 7)
-        group_channel(3, 1, "S", 256, 512)
-        weigh(0, 0, 3, "S")
-        group_channel(3, 1, "V", 0, 256)
-        stage1(5, 0, 1, 3, 6)
-        weigh(0, 0, 0, "S")
-        stage1(5, 1, 1, 2, 4)
-        weigh(0, 1, 2, "V")
-        stage1(4, 1, 1, 1, 1)
-        weigh(0, 1, 1, "S")
-        quant_channel(2, 1)
-        stage1(5, 1, 1, 1, 1)
-        weigh(0, 1, 0, "S")
-        stage1(5, 1, 1, 0, 0)
-        stage1(5, 1, 1, 3, 7)
-        stage1(4, 1, 1, 3, 7)
-        load_channel(1, 1)
-        stage1(2, 1, 1, 2, 4)
-        quant_channel(3, 1)
-        group_channel(1, 1, "V", 0, 256)
-        weigh(0, 1, 3, "S")
-        group_vw(0, 1, "V", 256, 512)
-        load_channel(0, 1)
-        stage1(2, 1, 1, 3, 7)
-        stage1(3, 1, 1, 1, 1)
-        group_channel(1, 1, "S", 256, 512)
-        weigh(0, 0, 1, "S")
-        quant_channel(1, 1)
-        weigh(0, 0, 2, "S")
-        stage1(2, 1, 1, 0, 0)
-        load_precoder(0)
-        group_channel(0, 1, "V", 0, 256)
-        load_precoder(1)
-        load_extra(1, 0)
-        group_vw(0, 0, "V", 0, 256)
-        stage1(3, 1, 1, 0, 0)
-        stage1(3, 1, 1, 3, 7)
-        stage1(3, 1, 1, 2, 4)
-        turn_precoder(0, 1, 1, 5)
-        group_precoder(0, 1, 1, "S")
-        turn_precoder(0, 1, 0, 6)
-        gains_turn(3)
-        gains_cols()
-        group_vw(0, 1, "V", 0, 256)
-        turn_precoder(0, 0, 0, 2)
-        group_precoder(0, 1, 0, "S")
-        group_precoder(0, 0, 0, "S")
-        group_channel(0, 1, "V", 256, 512)
-        quant_vw(0, 1)
-        turn_precoder(0, 0, 1, 5)
-        turn_precoder(1, 1, 0, 3)
-        quant_precoder(0, 1)
-        group_precoder(0, 0, 1, "S")
-        quant_precoder(0, 0)
-        group_vw(0, 0, "S", 256, 512)
-        turn_precoder(1, 0, 1, 6)
-        turn_precoder(1, 1, 1, 2)
-        turn_precoder(1, 0, 0, 5)
-        stage1(4, 1, 1, 0, 0)
-        stage1(1, 1, 1, 0, 0)
-        quant_vw(0, 0)
-        group_precoder(1, 0, 1, "S")
-        stage1(1, 1, 1, 1, 1)
-        group_precoder(1, 0, 0, "S")
-        quant_channel(0, 1)
-        stage2(2, 0, 6)
-        stage2(3, 0, 5)
-        quant_precoder(1, 0)
-        group_precoder(1, 1, 0, "S")
-        stage1(0, 1, 1, 0, 0)
-        load_extra(0, 0)
-        add_extra(2, 0)
-        stage2(1, 0, 3)
-        add_extra(3, 0)
-        stage2(0, 0, 6)
-        finish_y(2, 0)
-        stage1(4, 1, 1, 2, 4)
-        stage1(1, 1, 1, 2, 4)
-        group_precoder(1, 1, 1, "S")
-        stage1(0, 1, 1, 2, 4)
-        quant_precoder(1, 1)
-        load_extra(0, 1)
-        finish_y(3, 0)
-        add_extra(1, 0)
-        stage1(2, 1, 1, 1, 1)
-        add_extra(0, 0)
-        finish_y(1, 0)
-        stage2(3, 1, 2)
-        add_extra(3, 1)
-        load_extra(1, 1)
-        round_y(2, 0, "S")
-        round_y(3, 0, "S")
-        weigh(1, 1, 2, "S")
-        stage1(0, 1, 1, 1, 1)
-        stage2(1, 1, 5)
-        weigh(1, 1, 0, "S")
-        store_y(2, 0)
-        weigh(1, 1, 1, "S")
-        turn_y(2, 2, 0, 3)
-        finish_y(3, 1)
-        group_y(2, 2, 0, "S")
-        round_y(1, 0, "S")
-        stage1(1, 1, 1, 3, 7)
-        stage1(0, 1, 1, 3, 7)
-        stage2(0, 1, 6)
-        weigh(1, 1, 3, "S")
-        group_vw(1, 1, "S", 0, 256)
-        stage1(1, 1, 0, 1, 4)
-        add_extra(1, 1)
-        finish_y(1, 1)
-        store_y(3, 0)
-        quant_y(2, 2, 0)
-        stage1(5, 1, 0, 1, 4)
-        store_y(1, 1)
-        stage1(2, 1, 0, 3, 0)
-        finish_y(0, 0)
-        store_y(0, 0)
-        stage1(3, 1, 0, 0, 2)
-        add_extra(0, 1)
-        finish_y(0, 1)
-        stage2(2, 1, 1)
-        add_extra(2, 1)
-        stage1(5, 1, 0, 3, 0)
-        finish_y(2, 1)
-        stage1(4, 1, 0, 3, 0)
-        round_y(1, 1, "S")
-        stage1(4, 1, 0, 0, 2)
-        stage1(0, 1, 0, 1, 4)
-        stage1(3, 1, 0, 1, 4)
-        round_y(3, 1, "S")
-        group_vw(1, 1, "V", 256, 512)
-        stage1(0, 1, 0, 0, 2)
-        stage1(3, 1, 0, 3, 0)
-        stage1(0, 1, 0, 3, 0)
-        store_y(0, 1)
-        round_y(2, 1, "V")
-        stage1(1, 1, 0, 3, 0)
-        round_y(0, 0, "S")
-        stage1(1, 1, 0, 0, 2)
-        weigh(1, 0, 3, "S")
-        stage1(2, 1, 0, 0, 2)
-        stage1(0, 1, 0, 2, 3)
-        store_codes(2, 2, 0)
-        quant_vw(1, 1)
-        stage1(5, 1, 0, 2, 3)
-        stage1(3, 1, 0, 2, 3)
-        stage1(4, 1, 0, 2, 3)
-        stage1(2, 1, 0, 2, 3)
-        stage1(1, 1, 0, 2, 3)
+        stage1(5, 0, 0, 2, 0)
+        stage1(5, 0, 0, 1, 2)
+        stage1(5, 0, 0, 3, 6)
+        stage1(5, 1, 0, 3, 3)
+        load_wide(3, 0)
+        load_wide(4, 0)
+        stage1(5, 0, 0, 0, 4)
+        group_channel(2, 0, "S", 256, 512)
+        stage1(5, 1, 0, 0, 7)
+        quant_channel(2, 0, 2)
+        load_channel(3)
+        group_wide(2, 0, "S")
+        quant_wide(2, 0)
+        stage1(2, 0, 0, 1, 2)
+        stage1(2, 1, 0, 0, 7)
+        stage1(5, 1, 0, 1, 1)
+        group_wide(3, 0, "S")
+        stage1(2, 0, 0, 2, 0)
+        stage1(2, 0, 0, 0, 4)
+        group_wide(4, 0, "V")
+        stage1(2, 1, 0, 3, 3)
+        stage1(5, 1, 0, 2, 5)
+        quant_wide(4, 0)
+        stage1(2, 1, 0, 1, 1)
+        stage1(2, 1, 0, 2, 5)
+        load_codebook(0)
+        stage1(4, 0, 0, 2, 0)
+        stage1(4, 1, 0, 3, 3)
+        stage1(4, 1, 0, 2, 5)
+        stage1(4, 1, 0, 1, 1)
+        group_channel(3, 0, "S", 0, 256)
+        stage1(4, 1, 0, 0, 7)
+        stage1(4, 0, 0, 1, 2)
+        stage1(4, 0, 0, 3, 6)
+        stage1(4, 0, 0, 0, 4)
+        group_channel(3, 0, "S", 256, 512)
+        stage1(2, 0, 0, 3, 6)
+        group_channel(3, 1, "V", 0, 512)
+        quant_channel(3, 1, 1)
+        quant_wide(3, 0)
+        stage1(3, 1, 0, 2, 5)
+        stage1(3, 1, 0, 1, 1)
+        stage1(3, 1, 0, 3, 3)
+        stage1(3, 1, 0, 0, 7)
+        load_wide(0, 1)
+        load_wide(3, 1)
+        group_wide(0, 1, "S")
         weigh(1, 0, 2, "S")
-        stage1(5, 1, 0, 0, 2)
-        stage1(4, 1, 0, 1, 4)
-        stage1(2, 1, 0, 1, 4)
-        weigh(1, 0, 1, "S")
-        weigh(1, 0, 0, "V")
-        turn_y(0, 2, 0, 5)
-        round_y(0, 1, "V")
-        group_y(0, 2, 0, "S")
-        store_y(2, 1)
-        store_y(3, 1)
-        turn_y(0, 2, 1, 7)
-        group_y(0, 2, 1, "S")
-        group_vw(1, 0, "V", 0, 256)
-        turn_y(2, 2, 1, 6)
-        group_vw(1, 0, "V", 256, 512)
-        quant_vw(1, 0)
-        store_y(1, 0)
-        stage2(7, 0, 1)
-        quant_y(0, 2, 0)
-        quant_y(0, 2, 1)
-        group_y(2, 2, 1, "S")
-        quant_y(2, 2, 1)
-        store_codes(2, 2, 1)
-        stage2(6, 0, 0)
-        store_scales(0, [nc.sync] * 4)
-        store_codes(0, 2, 0)
-        add_extra(7, 0)
-        stage2(6, 1, 3)
-        add_extra(6, 0)
-        finish_y(7, 0)
-        store_y(7, 0)
-        round_y(7, 0, "S")
-        stage2(4, 1, 2)
+        quant_channel(3, 0, 1)
+        stage1(3, 0, 0, 1, 2)
+        group_wide(3, 1, "V")
+        load_precoder(0)
+        weigh(1, 0, 1, "V")
+        weigh(0, 0, 1, "S")
+        stage1(3, 0, 0, 0, 4)
+        stage1(3, 0, 0, 3, 6)
+        stage1(3, 0, 0, 2, 0)
+        weigh(0, 0, 3, "S")
+        quant_wide(3, 1)
+        gains_turn(1)
+        gains_cols()
+        quant_wide(0, 1)
+        turn_precoder(0, 0, 0, 5)
+        weigh(0, 0, 0, "S")
+        group_precoder(0, 0, 0, "V")
+        turn_precoder(0, 1, 1, 1)
+        load_wide(4, 1)
+        group_wide(4, 1, "V")
+        load_wide(2, 1)
+        stage1(0, 0, 1, 1, 2)
+        turn_precoder(0, 1, 0, 6)
+        weigh(0, 0, 2, "S")
+        group_precoder(0, 1, 0, "S")
+        turn_precoder(0, 0, 1, 5)
+        group_wide(2, 1, "V")
+        group_precoder(0, 0, 1, "S")
+        stage1(0, 0, 1, 2, 4)
+        stage1(3, 0, 1, 1, 2)
+        load_wide(5, 1)
+        stage1(3, 0, 1, 2, 4)
+        stage1(3, 0, 1, 0, 0)
+        stage1(3, 0, 1, 3, 6)
+        quant_wide(4, 1)
+        stage1(3, 1, 1, 0, 5)
+        stage1(0, 0, 1, 0, 0)
+        load_wide(1, 1)
+        group_wide(5, 1, "S")
+        quant_wide(2, 1)
+        stage1(0, 0, 1, 3, 6)
+        stage1(4, 0, 1, 1, 2)
+        stage1(4, 0, 1, 3, 6)
+        stage1(2, 0, 1, 2, 4)
+        stage1(0, 1, 1, 0, 5)
+        stage1(2, 0, 1, 0, 0)
+        stage1(2, 0, 1, 1, 2)
+        stage1(4, 0, 1, 2, 4)
+        stage1(4, 0, 1, 0, 0)
+        group_precoder(0, 1, 1, "S")
+        group_wide(1, 1, "V")
+        group_vw(0, 0, "S", 0, 512)
+        quant_wide(5, 1)
+        quant_wide(1, 1)
+        quant_precoder(0)
+        stage1(2, 0, 1, 3, 6)
+        stage1(5, 0, 1, 0, 0)
+        stage1(5, 0, 1, 3, 6)
+        stage1(5, 0, 1, 2, 4)
+        stage1(1, 0, 1, 3, 6)
+        load_precoder(1)
+        weigh(0, 1, 3, "S")
+        stage1(1, 0, 1, 0, 0)
+        weigh(0, 1, 0, "V")
+        stage1(5, 0, 1, 1, 2)
+        stage1(1, 0, 1, 2, 4)
+        stage1(1, 0, 1, 1, 2)
+        weigh(0, 1, 1, "S")
+        turn_precoder(1, 1, 0, 1)
+        group_precoder(1, 1, 0, "S")
+        weigh(0, 1, 2, "V")
+        turn_precoder(1, 1, 1, 0)
+        group_precoder(1, 1, 1, "S")
+        stage1(3, 1, 1, 2, 6)
+        turn_precoder(1, 0, 1, 4)
+        group_precoder(1, 0, 1, "S")
+        turn_precoder(1, 0, 0, 2)
+        group_precoder(1, 0, 0, "S")
+        stage1(2, 1, 1, 2, 6)
+        quant_vw(0, 0, 1)
+        stage1(1, 1, 1, 0, 5)
+        group_vw(0, 1, "V", 0, 256)
+        group_vw(0, 1, "V", 256, 512)
+        quant_vw(0, 1, 1)
+        quant_precoder(1)
+        stage1(5, 1, 1, 1, 1)
+        stage2(0, 0, 0)
+        weigh(1, 0, 0, "S")
+        stage2(1, 0, 4)
+        load_extra(0)
+        stage1(2, 1, 1, 0, 5)
+        add_extra(1, 0)
+        weigh(1, 0, 3, "S")
+        stage1(0, 1, 1, 3, 2)
+        add_extra(0, 0)
+        load_extra(1)
+        stage2(1, 1, 7)
+        add_extra(1, 1)
+        stage2(0, 1, 3)
+        add_extra(0, 1)
+        group_vw(1, 0, "S", 0, 512)
+        stage1(5, 1, 1, 0, 5)
+        stage1(4, 1, 1, 0, 5)
+        stage2(2, 1, 4)
+        weigh(1, 1, 0, "S")
+        finish_y(1, 0, 2, "V")
+        round_y(1, 0, "S")
+        finish_y(0, 0, 2, "V")
+        round_y(1, 1, "S")
+        round_y(0, 0, "S")
+        stage1(0, 1, 1, 2, 6)
+        stage1(1, 1, 1, 3, 2)
+        round_y(0, 1, "S")
+        stage2(2, 0, 0)
+        add_extra(2, 0)
+        stage1(5, 1, 1, 2, 6)
+        add_extra(2, 1)
+        stage1(3, 1, 1, 1, 1)
+        quant_vw(1, 0, 1)
+        finish_y(2, 0, 2, "V")
+        stage1(1, 1, 1, 2, 6)
+        stage1(4, 1, 1, 3, 2)
+        stage1(2, 1, 1, 1, 1)
+        stage1(4, 1, 1, 1, 1)
+        stage1(1, 1, 1, 1, 1)
+        stage1(0, 1, 1, 1, 1)
+        weigh(1, 1, 1, "S")
+        stage1(4, 1, 1, 2, 6)
+        weigh(1, 1, 2, "S")
+        stage1(5, 1, 1, 3, 2)
+        stage1(3, 1, 1, 3, 2)
+        stage1(2, 1, 1, 3, 2)
+        stage2(3, 1, 7)
+        add_extra(3, 1)
+        weigh(1, 1, 3, "S")
+        group_vw(1, 1, "V", 256, 512)
+        stage2(3, 0, 3)
+        add_extra(3, 0)
+        group_vw(1, 1, "S", 0, 256)
+        quant_vw(1, 1, 1)
+        turn_y(1, 0, 2, 5)
+        group_y(1, 0, 2, "S")
+        round_y(2, 1, "S")
+        store_y(1, 0, 2)
+        store_y(2, 0, 2)
+        round_y(2, 0, "S")
+        turn_y(0, 0, 2, 0)
+        stage2(4, 1, 4)
+        finish_y(3, 0, 2, "V")
+        stage2(4, 0, 1)
+        round_y(3, 1, "S")
+        store_y(0, 0, 2)
         add_extra(4, 1)
-        finish_y(6, 0)
-        round_y(6, 0, "S")
-        finish_y(4, 1)
-        round_y(4, 1, "S")
-        stage2(5, 1, 4)
-        add_extra(5, 1)
-        stage2(4, 0, 5)
         add_extra(4, 0)
-        finish_y(5, 1)
-        finish_y(4, 0)
-        store_y(6, 0)
-        turn_y(6, 2, 0, 7)
-        group_y(6, 2, 0, "S")
-        stage2(5, 0, 6)
-        round_y(5, 1, "S")
-        store_y(4, 1)
-        turn_y(4, 2, 1, 1)
+        round_y(3, 0, "S")
+        stage2(5, 1, 6)
+        add_extra(5, 1)
+        stage2(5, 0, 2)
         add_extra(5, 0)
-        store_codes(0, 2, 1)
-        round_y(4, 0, "S")
+        turn_y(2, 0, 2, 7)
+        group_y(0, 0, 2, "S")
+        quant_y(0, 2, 1)
+        store_y(3, 0, 2)
+        group_y(2, 0, 2, "S")
+        turn_y(3, 0, 2, 3)
+        group_y(3, 0, 2, "S")
+        finish_y(5, 0, 2, "V")
+        store_y(5, 0, 2)
+        quant_y(2, 2, 1)
+        round_y(5, 1, "S")
+        store_codes(0, 4, 1)
+        finish_y(4, 0, 2, "V")
+        stage2(6, 1, 5)
+        quant_y(0, 2, 0)
+        stage2(7, 0, 4)
         add_extra(6, 1)
-        finish_y(5, 0)
+        stage2(6, 0, 1)
+        add_extra(6, 0)
+        quant_y(2, 2, 0)
+        store_codes(0, 4, 0)
+        store_y(4, 0, 2)
         round_y(5, 0, "S")
-        store_y(4, 0)
-        store_y(5, 1)
-        finish_y(6, 1)
-        store_y(6, 1)
-        stage2(7, 1, 0)
+        store_scales(0, [nc.sync] * 4)
+        finish_y(6, 0, 2, "V")
+        store_y(6, 0, 2)
+        stage2(7, 1, 6)
         add_extra(7, 1)
-        turn_y(4, 2, 0, 2)
+        add_extra(7, 0)
+        finish_y(7, 1, 1, "V")
+        finish_y(7, 0, 1, "V")
+        round_y(4, 1, "S")
+        turn_y(5, 0, 2, 0)
+        group_y(5, 0, 2, "S")
+        store_y(7, 1, 1)
+        round_y(4, 0, "S")
+        turn_y(4, 0, 2, 2)
+        group_y(4, 0, 2, "S")
         round_y(6, 1, "S")
-        turn_y(6, 1, 1, 4)
-        quant_y(6, 2, 0)
-        finish_y(7, 1)
-        round_y(7, 1, "V")
-        group_y(4, 2, 0, "S")
-        group_y(4, 2, 1, "S")
-        store_y(5, 0)
-        group_y(6, 1, 1, "S")
-        store_codes(6, 2, 0)
         quant_y(4, 2, 0)
-        store_codes(4, 2, 0)
+        round_y(7, 0, "V")
+        round_y(6, 0, "S")
+        turn_y(6, 0, 2, 7)
         quant_y(4, 2, 1)
-        store_codes(4, 2, 1)
+        round_y(7, 1, "S")
+        turn_y(7, 1, 1, 3)
+        group_y(6, 0, 2, "S")
         quant_y(6, 1, 1)
-        turn_y(7, 1, 1, 5)
         group_y(7, 1, 1, "S")
-        store_y(7, 1)
+        quant_y(6, 1, 0)
+        turn_y(7, 0, 1, 5)
+        store_y(7, 0, 1)
+        store_codes(4, 2, 0)
         quant_y(7, 1, 1)
-        store_scales(1, [nc.sync] * 4)
+        store_codes(4, 2, 1)
         store_codes(6, 2, 1)
+        group_y(7, 0, 1, "S")
+        quant_y(7, 1, 0)
+        store_scales(1, [nc.sync] * 4)
+        store_codes(6, 2, 0)

@@ -298,315 +298,322 @@ def tile_weighted_transmit_covariance_block_k6_kernel(
         def gains_rows(engine):
             copy_on(engine, gain2_rows[:].rearrange("q (p j) -> q p j", j=8), T["spread"][:].rearrange("q (j p) -> q p j", j=8))
 
-        load_channel(1)
         gains_spread(0)
+        load_channel(1)
+        load_wide(1, 0)
+        group_channel(1, 0, "S", 0, 256)
         gains_rows("V")
         group_channel(1, 1, "V", 0, 512)
-        load_wide(1, 0)
         group_wide(1, 0, "V")
         group_channel(1, 0, "S", 256, 512)
-        quant_wide(1, 0)
-        group_channel(1, 0, "S", 0, 256)
         quant_channel(1, 0, 2)
-        stage1(1, 1, 0, 1, 1)
-        stage1(1, 0, 0, 1, 2)
-        stage1(1, 1, 0, 3, 3)
-        load_channel_half(0, 0)
-        load_channel_half(0, 1)
-        stage1(1, 0, 0, 0, 4)
-        group_channel(0, 0, "S", 0, 256)
-        group_channel(0, 0, "S", 256, 512)
-        group_channel(0, 1, "S", 0, 512)
-        quant_channel(0, 0, 1)
-        stage1(1, 1, 0, 2, 5)
-        load_wide(0, 0)
-        group_wide(0, 0, "V")
-        quant_wide(0, 0)
-        stage1(0, 0, 0, 1, 2)
-        stage1(0, 0, 0, 0, 4)
-        stage1(1, 0, 0, 3, 6)
-        stage1(0, 0, 0, 3, 6)
-        quant_channel(0, 1, 1)
-        stage1(0, 1, 0, 0, 7)
-        load_wide(5, 0)
-        load_channel(2)
-        stage1(0, 1, 0, 1, 1)
-        stage1(0, 0, 0, 2, 0)
+        quant_wide(1, 0)
+        stage1(1, 1, 0, 2, 1)
+        stage1(1, 0, 0, 0, 2)
+        stage1(1, 0, 0, 2, 3)
+        stage1(1, 0, 0, 1, 4)
+        stage1(1, 0, 0, 3, 5)
         load_wide(2, 0)
-        stage1(0, 1, 0, 3, 3)
-        group_wide(5, 0, "S")
-        stage1(0, 1, 0, 2, 5)
-        widen_weights()
-        group_channel(2, 0, "V", 0, 256)
-        quant_wide(5, 0)
-        stage1(1, 1, 0, 0, 7)
-        stage1(1, 0, 0, 2, 0)
-        group_channel(2, 1, "V", 0, 512)
-        load_codebook(1)
-        stage1(5, 0, 0, 2, 0)
-        stage1(5, 0, 0, 1, 2)
-        stage1(5, 0, 0, 3, 6)
-        stage1(5, 1, 0, 3, 3)
-        load_wide(3, 0)
-        load_wide(4, 0)
-        stage1(5, 0, 0, 0, 4)
-        group_channel(2, 0, "S", 256, 512)
-        stage1(5, 1, 0, 0, 7)
-        quant_channel(2, 0, 2)
-        load_channel(3)
         group_wide(2, 0, "S")
         quant_wide(2, 0)
-        stage1(2, 0, 0, 1, 2)
-        stage1(2, 1, 0, 0, 7)
-        stage1(5, 1, 0, 1, 1)
-        group_wide(3, 0, "S")
-        stage1(2, 0, 0, 2, 0)
-        stage1(2, 0, 0, 0, 4)
-        group_wide(4, 0, "V")
-        stage1(2, 1, 0, 3, 3)
-        stage1(5, 1, 0, 2, 5)
-        quant_wide(4, 0)
-        stage1(2, 1, 0, 1, 1)
-        stage1(2, 1, 0, 2, 5)
-        load_codebook(0)
-        stage1(4, 0, 0, 2, 0)
-        stage1(4, 1, 0, 3, 3)
-        stage1(4, 1, 0, 2, 5)
-        stage1(4, 1, 0, 1, 1)
-        group_channel(3, 0, "S", 0, 256)
-        stage1(4, 1, 0, 0, 7)
-        stage1(4, 0, 0, 1, 2)
-        stage1(4, 0, 0, 3, 6)
-        stage1(4, 0, 0, 0, 4)
+        load_channel(2)
+        group_channel(2, 0, "V", 256, 512)
+        load_wide(5, 0)
+        group_channel(2, 1, "V", 0, 512)
+        group_channel(2, 0, "S", 0, 256)
+        quant_channel(2, 0, 2)
+        stage1(2, 0, 0, 0, 2)
+        load_channel(3)
+        load_codebook(1)
+        group_wide(5, 0, "S")
+        quant_wide(5, 0)
+        stage1(5, 1, 0, 3, 6)
+        stage1(5, 1, 0, 2, 1)
+        stage1(5, 1, 0, 1, 7)
+        stage1(2, 0, 0, 2, 3)
+        stage1(1, 1, 0, 3, 6)
+        stage1(5, 1, 0, 0, 0)
+        stage1(5, 0, 0, 3, 5)
+        widen_weights()
+        stage1(2, 0, 0, 3, 5)
+        stage1(5, 0, 0, 2, 3)
+        load_wide(3, 0)
+        group_channel(3, 0, "V", 0, 256)
+        stage1(2, 1, 0, 2, 1)
+        stage1(2, 1, 0, 1, 7)
+        load_wide(0, 0)
+        stage1(2, 0, 0, 1, 4)
+        stage1(1, 1, 0, 0, 0)
         group_channel(3, 0, "S", 256, 512)
-        stage1(2, 0, 0, 3, 6)
-        group_channel(3, 1, "V", 0, 512)
-        quant_channel(3, 1, 1)
-        quant_wide(3, 0)
-        stage1(3, 1, 0, 2, 5)
-        stage1(3, 1, 0, 1, 1)
-        stage1(3, 1, 0, 3, 3)
-        stage1(3, 1, 0, 0, 7)
-        load_wide(0, 1)
-        load_wide(3, 1)
-        group_wide(0, 1, "S")
-        weigh(1, 0, 2, "S")
+        group_wide(3, 0, "V")
         quant_channel(3, 0, 1)
-        stage1(3, 0, 0, 1, 2)
-        group_wide(3, 1, "V")
-        load_precoder(0)
-        weigh(1, 0, 1, "V")
-        weigh(0, 0, 1, "S")
-        stage1(3, 0, 0, 0, 4)
-        stage1(3, 0, 0, 3, 6)
-        stage1(3, 0, 0, 2, 0)
-        weigh(0, 0, 3, "S")
-        quant_wide(3, 1)
-        gains_turn(1)
-        gains_cols()
-        quant_wide(0, 1)
-        turn_precoder(0, 0, 0, 5)
-        weigh(0, 0, 0, "S")
-        group_precoder(0, 0, 0, "V")
-        turn_precoder(0, 1, 1, 1)
-        load_wide(4, 1)
-        group_wide(4, 1, "V")
+        stage1(5, 0, 0, 0, 2)
+        quant_wide(3, 0)
+        stage1(3, 0, 0, 0, 2)
+        stage1(3, 0, 0, 3, 5)
+        stage1(1, 1, 0, 1, 7)
+        load_wide(4, 0)
+        load_codebook(0)
+        group_channel(3, 1, "S", 0, 512)
+        quant_channel(3, 1, 1)
+        stage1(3, 1, 0, 1, 7)
+        stage1(3, 1, 0, 2, 1)
+        stage1(3, 0, 0, 1, 4)
+        stage1(2, 1, 0, 3, 6)
+        stage1(2, 1, 0, 0, 0)
+        stage1(3, 0, 0, 2, 3)
+        group_wide(4, 0, "V")
+        stage1(3, 1, 0, 3, 6)
+        load_channel_half(0, 1)
+        stage1(3, 1, 0, 0, 0)
+        load_channel_half(0, 0)
+        group_wide(0, 0, "S")
+        quant_wide(0, 0)
+        quant_wide(4, 0)
+        stage1(4, 0, 0, 3, 5)
+        stage1(4, 1, 0, 3, 6)
+        stage1(4, 0, 0, 1, 4)
+        stage1(5, 0, 0, 1, 4)
+        stage1(4, 0, 0, 2, 3)
+        stage1(4, 0, 0, 0, 2)
+        group_channel(0, 0, "V", 0, 256)
+        group_channel(0, 1, "S", 0, 512)
+        load_wide(3, 1)
+        group_channel(0, 0, "V", 256, 512)
+        quant_channel(0, 1, 1)
+        stage1(4, 1, 0, 1, 7)
+        stage1(4, 1, 0, 2, 1)
+        stage1(0, 1, 0, 0, 0)
+        stage1(0, 1, 0, 3, 6)
+        stage1(0, 1, 0, 2, 1)
+        stage1(4, 1, 0, 0, 0)
+        stage1(0, 1, 0, 1, 7)
+        quant_channel(0, 0, 1)
+        stage1(0, 0, 0, 0, 2)
+        stage1(0, 0, 0, 2, 3)
+        stage1(0, 0, 0, 1, 4)
+        stage1(0, 0, 0, 3, 5)
         load_wide(2, 1)
-        stage1(0, 0, 1, 1, 2)
-        turn_precoder(0, 1, 0, 6)
-        weigh(0, 0, 2, "S")
-        group_precoder(0, 1, 0, "S")
-        turn_precoder(0, 0, 1, 5)
+        group_wide(3, 1, "S")
+        load_precoder(0)
         group_wide(2, 1, "V")
-        group_precoder(0, 0, 1, "S")
-        stage1(0, 0, 1, 2, 4)
-        stage1(3, 0, 1, 1, 2)
-        load_wide(5, 1)
-        stage1(3, 0, 1, 2, 4)
-        stage1(3, 0, 1, 0, 0)
-        stage1(3, 0, 1, 3, 6)
-        quant_wide(4, 1)
-        stage1(3, 1, 1, 0, 5)
-        stage1(0, 0, 1, 0, 0)
-        load_wide(1, 1)
-        group_wide(5, 1, "S")
-        quant_wide(2, 1)
-        stage1(0, 0, 1, 3, 6)
-        stage1(4, 0, 1, 1, 2)
-        stage1(4, 0, 1, 3, 6)
-        stage1(2, 0, 1, 2, 4)
-        stage1(0, 1, 1, 0, 5)
-        stage1(2, 0, 1, 0, 0)
-        stage1(2, 0, 1, 1, 2)
-        stage1(4, 0, 1, 2, 4)
-        stage1(4, 0, 1, 0, 0)
-        group_precoder(0, 1, 1, "S")
-        group_wide(1, 1, "V")
-        group_vw(0, 0, "S", 0, 512)
-        quant_wide(5, 1)
-        quant_wide(1, 1)
-        quant_precoder(0)
-        stage1(2, 0, 1, 3, 6)
-        stage1(5, 0, 1, 0, 0)
-        stage1(5, 0, 1, 3, 6)
-        stage1(5, 0, 1, 2, 4)
-        stage1(1, 0, 1, 3, 6)
-        load_precoder(1)
-        weigh(0, 1, 3, "S")
-        stage1(1, 0, 1, 0, 0)
-        weigh(0, 1, 0, "V")
-        stage1(5, 0, 1, 1, 2)
-        stage1(1, 0, 1, 2, 4)
-        stage1(1, 0, 1, 1, 2)
-        weigh(0, 1, 1, "S")
-        turn_precoder(1, 1, 0, 1)
-        group_precoder(1, 1, 0, "S")
-        weigh(0, 1, 2, "V")
-        turn_precoder(1, 1, 1, 0)
-        group_precoder(1, 1, 1, "S")
-        stage1(3, 1, 1, 2, 6)
-        turn_precoder(1, 0, 1, 4)
-        group_precoder(1, 0, 1, "S")
-        turn_precoder(1, 0, 0, 2)
-        group_precoder(1, 0, 0, "S")
-        stage1(2, 1, 1, 2, 6)
-        quant_vw(0, 0, 1)
-        stage1(1, 1, 1, 0, 5)
-        group_vw(0, 1, "V", 0, 256)
-        group_vw(0, 1, "V", 256, 512)
-        quant_vw(0, 1, 1)
-        quant_precoder(1)
-        stage1(5, 1, 1, 1, 1)
-        stage2(0, 0, 0)
-        weigh(1, 0, 0, "S")
-        stage2(1, 0, 4)
-        load_extra(0)
-        stage1(2, 1, 1, 0, 5)
-        add_extra(1, 0)
+        quant_wide(3, 1)
         weigh(1, 0, 3, "S")
-        stage1(0, 1, 1, 3, 2)
-        add_extra(0, 0)
-        load_extra(1)
-        stage2(1, 1, 7)
-        add_extra(1, 1)
-        stage2(0, 1, 3)
-        add_extra(0, 1)
-        group_vw(1, 0, "S", 0, 512)
-        stage1(5, 1, 1, 0, 5)
-        stage1(4, 1, 1, 0, 5)
-        stage2(2, 1, 4)
-        weigh(1, 1, 0, "S")
-        finish_y(1, 0, 2, "V")
-        round_y(1, 0, "S")
-        finish_y(0, 0, 2, "V")
-        round_y(1, 1, "S")
-        round_y(0, 0, "S")
-        stage1(0, 1, 1, 2, 6)
-        stage1(1, 1, 1, 3, 2)
-        round_y(0, 1, "S")
-        stage2(2, 0, 0)
+        weigh(1, 0, 0, "S")
+        weigh(1, 0, 1, "S")
+        weigh(0, 0, 2, "V")
+        load_wide(1, 1)
+        stage1(3, 0, 1, 0, 6)
+        weigh(0, 0, 3, "S")
+        turn_precoder(0, 1, 1, 0)
+        group_precoder(0, 1, 1, "S")
+        turn_precoder(0, 1, 0, 3)
+        stage1(3, 0, 1, 2, 7)
+        load_wide(5, 1)
+        quant_wide(2, 1)
+        stage1(2, 0, 1, 2, 7)
+        turn_precoder(0, 0, 1, 5)
+        turn_precoder(0, 0, 0, 0)
+        group_precoder(0, 1, 0, "S")
+        group_wide(1, 1, "V")
+        stage1(2, 0, 1, 0, 6)
+        stage1(2, 0, 1, 3, 3)
+        stage1(3, 0, 1, 3, 3)
+        weigh(0, 0, 1, "S")
+        stage1(2, 1, 1, 2, 4)
+        weigh(0, 0, 0, "S")
+        stage1(2, 0, 1, 1, 2)
+        stage1(3, 1, 1, 2, 4)
+        stage1(3, 0, 1, 1, 2)
+        group_wide(5, 1, "V")
+        quant_wide(1, 1)
+        stage1(1, 0, 1, 2, 7)
+        stage1(1, 1, 1, 2, 4)
+        group_precoder(0, 0, 0, "S")
+        load_wide(0, 1)
+        stage1(1, 0, 1, 3, 3)
+        load_wide(4, 1)
+        group_wide(0, 1, "S")
+        quant_wide(5, 1)
+        stage1(1, 0, 1, 1, 2)
+        stage1(5, 0, 1, 2, 7)
+        stage1(5, 0, 1, 0, 6)
+        stage1(5, 0, 1, 3, 3)
+        stage1(1, 0, 1, 0, 6)
+        group_precoder(0, 0, 1, "S")
+        group_vw(0, 0, "S", 0, 512)
+        group_wide(4, 1, "V")
+        stage1(2, 1, 1, 3, 0)
+        stage1(5, 0, 1, 1, 2)
+        quant_wide(4, 1)
+        stage1(4, 0, 1, 2, 7)
+        stage1(4, 0, 1, 3, 3)
+        quant_wide(0, 1)
+        stage1(4, 0, 1, 1, 2)
+        stage1(0, 0, 1, 1, 2)
+        stage1(0, 0, 1, 2, 7)
+        weigh(0, 1, 1, "S")
+        quant_precoder(0)
+        stage1(0, 0, 1, 3, 3)
+        weigh(0, 1, 3, "S")
+        stage1(0, 0, 1, 0, 6)
+        weigh(0, 1, 2, "V")
+        load_precoder(1)
+        stage1(4, 0, 1, 0, 6)
+        quant_vw(0, 0, 1)
+        turn_precoder(1, 1, 0, 5)
+        weigh(0, 1, 0, "V")
+        turn_precoder(1, 1, 1, 7)
+        group_precoder(1, 1, 0, "S")
+        gains_turn(2)
+        stage1(3, 1, 1, 3, 0)
+        group_precoder(1, 1, 1, "S")
+        gains_cols()
+        turn_precoder(1, 0, 0, 3)
+        group_vw(0, 1, "V", 256, 512)
+        group_vw(0, 1, "V", 0, 256)
+        quant_vw(0, 1, 1)
+        turn_precoder(1, 0, 1, 6)
+        stage1(4, 1, 1, 2, 4)
+        group_precoder(1, 0, 0, "S")
+        group_precoder(1, 0, 1, "S")
+        quant_precoder(1)
+        stage1(4, 1, 1, 1, 2)
+        stage1(4, 1, 1, 3, 0)
+        stage1(0, 1, 1, 2, 4)
+        stage1(0, 1, 1, 3, 0)
+        load_extra(0)
+        stage2(2, 0, 5)
+        stage2(1, 0, 7)
+        weigh(1, 0, 2, "S")
         add_extra(2, 0)
-        stage1(5, 1, 1, 2, 6)
+        stage2(2, 1, 3)
+        finish_y(2, 0, 1, "G")
+        group_vw(1, 0, "S", 0, 512)
+        stage2(1, 1, 6)
+        stage1(5, 1, 1, 2, 4)
+        add_extra(1, 0)
+        stage1(1, 1, 1, 3, 0)
         add_extra(2, 1)
-        stage1(3, 1, 1, 1, 1)
-        quant_vw(1, 0, 1)
-        finish_y(2, 0, 2, "V")
-        stage1(1, 1, 1, 2, 6)
-        stage1(4, 1, 1, 3, 2)
-        stage1(2, 1, 1, 1, 1)
-        stage1(4, 1, 1, 1, 1)
-        stage1(1, 1, 1, 1, 1)
-        stage1(0, 1, 1, 1, 1)
-        weigh(1, 1, 1, "S")
-        stage1(4, 1, 1, 2, 6)
+        finish_y(2, 1, 1, "V")
+        finish_y(1, 0, 1, "G")
+        add_extra(1, 1)
+        stage2(3, 0, 1)
         weigh(1, 1, 2, "S")
-        stage1(5, 1, 1, 3, 2)
-        stage1(3, 1, 1, 3, 2)
-        stage1(2, 1, 1, 3, 2)
-        stage2(3, 1, 7)
-        add_extra(3, 1)
-        weigh(1, 1, 3, "S")
-        group_vw(1, 1, "V", 256, 512)
-        stage2(3, 0, 3)
         add_extra(3, 0)
-        group_vw(1, 1, "S", 0, 256)
-        quant_vw(1, 1, 1)
-        turn_y(1, 0, 2, 5)
-        group_y(1, 0, 2, "S")
         round_y(2, 1, "S")
-        store_y(1, 0, 2)
-        store_y(2, 0, 2)
+        finish_y(1, 1, 1, "V")
+        finish_y(3, 0, 1, "G")
+        stage2(3, 1, 5)
+        add_extra(3, 1)
+        stage1(3, 1, 1, 1, 2)
+        stage1(5, 1, 1, 3, 0)
+        stage1(0, 1, 1, 1, 2)
+        weigh(1, 1, 3, "V")
+        finish_y(3, 1, 1, "V")
         round_y(2, 0, "S")
-        turn_y(0, 0, 2, 0)
-        stage2(4, 1, 4)
-        finish_y(3, 0, 2, "V")
-        stage2(4, 0, 1)
+        stage1(5, 1, 1, 1, 2)
+        stage1(2, 1, 1, 1, 2)
+        load_extra(1)
+        round_y(1, 0, "S")
+        round_y(1, 1, "S")
+        stage1(1, 1, 1, 1, 2)
+        weigh(1, 1, 1, "S")
+        quant_vw(1, 0, 1)
+        store_y(2, 0, 2)
+        stage1(3, 1, 1, 0, 7)
+        stage1(5, 1, 1, 0, 7)
+        stage1(4, 1, 1, 0, 7)
+        stage1(1, 1, 1, 0, 7)
+        stage1(2, 1, 1, 0, 7)
+        stage1(0, 1, 1, 0, 7)
+        weigh(1, 1, 0, "S")
+        group_vw(1, 1, "V", 256, 512)
+        stage2(0, 0, 3)
+        group_vw(1, 1, "S", 0, 256)
+        store_y(1, 0, 2)
+        stage2(0, 1, 4)
+        add_extra(0, 1)
+        turn_y(2, 0, 2, 6)
+        quant_vw(1, 1, 1)
+        turn_y(1, 0, 2, 1)
+        stage2(5, 0, 5)
         round_y(3, 1, "S")
-        store_y(0, 0, 2)
-        add_extra(4, 1)
-        add_extra(4, 0)
-        round_y(3, 0, "S")
-        stage2(5, 1, 6)
-        add_extra(5, 1)
-        stage2(5, 0, 2)
-        add_extra(5, 0)
-        turn_y(2, 0, 2, 7)
-        group_y(0, 0, 2, "S")
-        quant_y(0, 2, 1)
+        add_extra(0, 0)
+        stage2(5, 1, 0)
         store_y(3, 0, 2)
+        finish_y(0, 1, 1, "V")
+        stage2(7, 0, 2)
+        add_extra(5, 0)
+        group_y(1, 0, 2, "S")
         group_y(2, 0, 2, "S")
-        turn_y(3, 0, 2, 3)
-        group_y(3, 0, 2, "S")
-        finish_y(5, 0, 2, "V")
+        round_y(3, 0, "S")
+        finish_y(0, 0, 1, "G")
+        round_y(0, 1, "S")
+        round_y(0, 0, "S")
+        store_y(0, 0, 2)
+        stage2(7, 1, 7)
+        add_extra(5, 1)
+        stage2(4, 1, 4)
+        finish_y(5, 0, 1, "V")
+        finish_y(5, 1, 1, "G")
+        turn_y(3, 0, 2, 1)
         store_y(5, 0, 2)
-        quant_y(2, 2, 1)
+        round_y(5, 0, "S")
+        add_extra(7, 1)
+        turn_y(0, 0, 2, 3)
+        group_y(0, 0, 2, "S")
+        stage2(4, 0, 6)
         round_y(5, 1, "S")
-        store_codes(0, 4, 1)
-        finish_y(4, 0, 2, "V")
-        stage2(6, 1, 5)
-        quant_y(0, 2, 0)
-        stage2(7, 0, 4)
+        stage2(6, 0, 5)
+        add_extra(7, 0)
+        stage2(6, 1, 0)
+        finish_y(7, 1, 1, "V")
+        store_y(7, 1, 1)
+        round_y(7, 1, "S")
+        finish_y(7, 0, 1, "G")
+        store_y(7, 0, 1)
+        add_extra(4, 0)
+        add_extra(4, 1)
+        finish_y(4, 0, 1, "V")
+        finish_y(4, 1, 1, "G")
+        store_y(4, 0, 2)
         add_extra(6, 1)
-        stage2(6, 0, 1)
         add_extra(6, 0)
+        quant_y(0, 2, 0)
+        turn_y(5, 0, 2, 7)
+        quant_y(0, 2, 1)
+        round_y(7, 0, "S")
+        group_y(3, 0, 2, "S")
         quant_y(2, 2, 0)
         store_codes(0, 4, 0)
-        store_y(4, 0, 2)
-        round_y(5, 0, "S")
-        store_scales(0, [nc.sync] * 4)
-        finish_y(6, 0, 2, "V")
-        store_y(6, 0, 2)
-        stage2(7, 1, 6)
-        add_extra(7, 1)
-        add_extra(7, 0)
-        finish_y(7, 1, 1, "V")
-        finish_y(7, 0, 1, "V")
-        round_y(4, 1, "S")
-        turn_y(5, 0, 2, 0)
-        group_y(5, 0, 2, "S")
-        store_y(7, 1, 1)
         round_y(4, 0, "S")
+        quant_y(2, 2, 1)
+        store_codes(0, 4, 1)
+        finish_y(6, 0, 1, "V")
+        finish_y(6, 1, 1, "V")
+        round_y(6, 1, "V")
+        round_y(4, 1, "S")
         turn_y(4, 0, 2, 2)
-        group_y(4, 0, 2, "S")
-        round_y(6, 1, "S")
-        quant_y(4, 2, 0)
-        round_y(7, 0, "V")
+        turn_y(7, 0, 1, 3)
+        group_y(5, 0, 2, "S")
         round_y(6, 0, "S")
-        turn_y(6, 0, 2, 7)
+        group_y(4, 0, 2, "S")
+        group_y(7, 0, 1, "V")
         quant_y(4, 2, 1)
-        round_y(7, 1, "S")
-        turn_y(7, 1, 1, 3)
-        group_y(6, 0, 2, "S")
-        quant_y(6, 1, 1)
+        quant_y(4, 2, 0)
+        turn_y(7, 1, 1, 6)
+        turn_y(6, 0, 2, 4)
         group_y(7, 1, 1, "S")
-        quant_y(6, 1, 0)
-        turn_y(7, 0, 1, 5)
-        store_y(7, 0, 1)
-        store_codes(4, 2, 0)
         quant_y(7, 1, 1)
-        store_codes(4, 2, 1)
-        store_codes(6, 2, 1)
-        group_y(7, 0, 1, "S")
+        store_scales(0, [nc.sync] * 4)
+        store_y(6, 0, 2)
+        store_codes(4, 2, 0)
         quant_y(7, 1, 0)
-        store_scales(1, [nc.sync] * 4)
+        group_y(6, 0, 2, "S")
+        store_codes(4, 2, 1)
+        quant_y(6, 1, 0)
         store_codes(6, 2, 0)
+        quant_y(6, 1, 1)
+        store_scales(1, [nc.sync] * 4)
+        store_codes(6, 2, 1)

from contextlib import ExitStack

import concourse.mybir as mybir
from concourse.masks import make_identity

M, N, R, L, U = 1024, 1024, 2048, 1024, 1024
FLOPS = 2 * M * U * (R + L) + 2 * M * N * U

F32 = mybir.dt.float32
BF16 = mybir.dt.bfloat16
U32 = mybir.dt.uint32
I32 = mybir.dt.int32
U8 = mybir.dt.uint8
FP8X4 = mybir.dt.float8_e4m3fn_x4
FP4X4 = mybir.dt.float4_e2m1fn_x4
COPY = mybir.ActivationFunctionType.Copy
MULT = mybir.AluOpType.mult
ADD = mybir.AluOpType.add

P = 128
HALF = 512
PASSES = [("h", 0), ("h", 1), ("h", 2), ("h", 3), ("c", 0), ("c", 1)]
GROUPED_BUFS = {1: 3, 2: 3}
WIDE_BUFS = 4
NARROW_BUFS = 5
VW_BUFS = 3
Y_BUFS = 3
SUM_BUFS = 2
RND_BUFS = 3
GY_BUFS = 2
WIDE_OUT = "p (t m j) -> p m j t"
WIDE_IN = "p j (m t) -> p m j t"


def tile_weighted_transmit_covariance_block_k6_kernel(
    tc, channel, coef, codebook_words, codebook_scales, beam_coef, user_weight, precoder2, gain1, extra, gain2,
    out_0, out_1, out_2,
):
    nc = tc.nc
    with ExitStack() as ctx:
        keep = ctx.enter_context(tc.tile_pool(name="keep", bufs=1))
        stage = ctx.enter_context(tc.tile_pool(name="stage", bufs=1))
        psum = ctx.enter_context(tc.psum_pool(name="psum", bufs=1))
        ctx.enter_context(tc.manual_schedule())
        T = {}

        def bank(b, shape, dtype, name):
            return psum.tile(shape, dtype, name=name, tag="bank%d" % b)

        def quantised(name, width):
            codes = keep.tile([P, width], U32, name=name + "_codes", align_bytes=64)
            scales = keep.tile([P, width], U8, name=name + "_scales", align_bytes=64)
            return codes, scales

        def grouped_tile(key, parts):
            if key not in T:
                name = "_".join(str(x) for x in key)
                T[key] = stage.tile([P, parts, 4 * HALF], BF16, name=name, tag="grouped%d" % parts, bufs=GROUPED_BUFS[parts], align_bytes=64)
            return T[key]

        def quantise_parts(kind, key, first, count, parts):
            if ("q" + kind,) + key not in T:
                T[("q" + kind,) + key] = quantised("q" + kind + "_".join(str(x) for x in key), HALF * parts)
            source = T[("g" + kind,) + key][:, first : first + count, :].rearrange("p a c -> p (a c)")
            quantise(T[("q" + kind,) + key], slice(HALF * first, HALF * (first + count)), source)

        def copy_on(engine, out, in_):
            if engine == "V":
                nc.vector.tensor_copy(out=out, in_=in_)
            else:
                nc.scalar.copy(out=out, in_=in_)

        def quantise(pair, cols, source):
            codes, scales = pair
            nc.vector.quantize_mx(out=codes[:, cols].bitcast(FP8X4), scales=scales[:, cols], in_=source)

        def load_wide(s, g):
            kind, k = PASSES[s]
            src = coef if kind == "h" else beam_coef
            raw = stage.tile([P, 4, HALF], BF16, name="wide%d_%d" % (s, g), tag="narrow", bufs=NARROW_BUFS)
            rows = src[HALF * k : HALF * (k + 1), HALF * g : HALF * (g + 1)]
            nc.sync.dma_start(out=raw[:], in_=rows.rearrange("(p j) u -> p j u", j=4))
            T["wide", s, g] = raw

        def load_channel(s):
            raw = stage.tile([P, 4, M], BF16, name="chan%d" % s, tag="wide", bufs=WIDE_BUFS)
            nc.sync.dma_start(out=raw[:], in_=channel[HALF * s : HALF * (s + 1), :].rearrange("(p j) m -> p j m", j=4))
            for mh in range(2):
                T["chan", s, mh] = raw[:, :, HALF * mh : HALF * (mh + 1)]

        def load_channel_half(s, mh):
            raw = stage.tile([P, 4, HALF], BF16, name="chan%d_%d" % (s, mh), tag="narrow", bufs=NARROW_BUFS)
            rows = channel[HALF * s : HALF * (s + 1), HALF * mh : HALF * (mh + 1)]
            nc.sync.dma_start(out=raw[:], in_=rows.rearrange("(p j) m -> p j m", j=4))
            T["chan", s, mh] = raw[:]

        def load_codebook(k):
            nc.sync.dma_start(out=book_words[:, k, :].bitcast(I32), in_=codebook_words[k].bitcast(I32))

        def load_precoder(nh):
            raw = stage.tile([P, 4, U], BF16, name="prec%d" % nh, tag="wide", bufs=WIDE_BUFS)
            nc.sync.dma_start(out=raw[:], in_=precoder2[HALF * nh : HALF * (nh + 1), :].rearrange("(j p) u -> p j u", p=P))
            T["prec", nh] = raw

        def load_extra(mh):
            raw = stage.tile([P, 4, N], BF16, name="extra%d" % mh, tag="wide", bufs=WIDE_BUFS)
            nc.sync.dma_start(out=raw[:], in_=extra[HALF * mh : HALF * (mh + 1), :].rearrange("(j p) n -> p j n", p=P))
            T["extra", mh] = raw

        def group_wide(s, g, engine):
            copy_on(
                engine,
                grouped_tile(("gw", s, g), 1)[:, 0, :].rearrange(WIDE_OUT, t=4, j=4),
                T["wide", s, g][:].rearrange(WIDE_IN, t=4),
            )

        def quant_wide(s, g):
            quantise_parts("w", (s, g), 0, 1, 1)

        def interleave(engine, grouped, rows, lo, hi):
            copy_on(
                engine,
                grouped[:, 4 * lo : 4 * hi].rearrange("p (c i j) -> p c j i", i=4, j=4),
                rows[:, :, lo:hi].rearrange("p j (c i) -> p c j i", i=4),
            )

        def group_channel(s, mh, engine, lo, hi):
            interleave(engine, grouped_tile(("gc", s), 2)[:, mh, :], T["chan", s, mh], lo, hi)

        def quant_channel(s, first, count):
            quantise_parts("c", (s,), first, count, 2)

        def stage1(s, mh, g, t, b):
            kind, k = PASSES[s]
            done = T.get(("passes", mh, g, t), 0)
            T["passes", mh, g, t] = done + 1
            if done == 0:
                T["acc1", mh, g, t] = bank(b, [P, HALF], F32, "acc1_%d_%d_%d" % (mh, g, t))
            codes, scales = T["qw", s, g]
            cols = slice(P * t, P * (t + 1))
            if kind == "h":
                rhs = T["qc", s][0][:, HALF * mh : HALF * (mh + 1)].bitcast(FP8X4)
                rhs_scale = T["qc", s][1][:, HALF * mh : HALF * (mh + 1)]
            else:
                rhs = book_words[:, k, 2 * HALF * mh : 2 * HALF * (mh + 1)].bitcast(FP4X4)
                rhs_scale = book_scales[:, k, HALF * mh : HALF * (mh + 1)]
            nc.tensor.matmul_mx(
                out=T["acc1", mh, g, t][:], lhsT=codes[:, cols].bitcast(FP8X4), lhsT_scale=scales[:, cols],
                rhs=rhs, rhs_scale=rhs_scale, start=(done == 0), stop=(done == len(PASSES) - 1),
            )

        def weigh(mh, g, t, engine):
            if ("vw", mh, g) not in T:
                T["vw", mh, g] = stage.tile([P, 4, HALF], BF16, name="vw%d_%d" % (mh, g), tag="vw", bufs=VW_BUFS)
            out = T["vw", mh, g][:, t, :]
            weight = weights[:, 4 * g + t : 4 * g + t + 1]
            if engine == "V":
                nc.vector.tensor_scalar(out=out, in0=T["acc1", mh, g, t][:], scalar1=weight, scalar2=None, op0=MULT)
            else:
                nc.scalar.activation(out=out, in_=T["acc1", mh, g, t][:], func=COPY, scale=weight)

        def group_vw(mh, g, engine, lo, hi):
            interleave(engine, grouped_tile(("gv", mh), 2)[:, g, :], T["vw", mh, g][:], lo, hi)

        def quant_vw(mh, first, count):
            quantise_parts("v", (mh,), first, count, 2)

        def turn_precoder(nh, g, jj, b):
            words = T["prec", nh][:].bitcast(F32)
            turned = bank(b, [P, 2, 2, P], F32, "pt%d_%d_%d" % (nh, g, jj))
            for j in range(2):
                for h in range(2):
                    nc.tensor.transpose(turned[:, j, h, :], words[:, 2 * jj + j, 256 * g + h : 256 * (g + 1) : 2], ident_f32[:])
            T["pt", nh, g, jj] = turned

        def group_precoder(nh, g, jj, engine):
            words = grouped_tile(("gp", nh), 2)[:, g, :].bitcast(F32)
            out = words[:, HALF * jj : HALF * (jj + 1)].rearrange("p (j r h) -> p j r h", j=2, h=2)
            copy_on(engine, out, T["pt", nh, g, jj][:].rearrange("p j h r -> p j r h"))

        def quant_precoder(nh):
            quantise_parts("p", (nh,), 0, 2, 2)

        def stage2(mt, nh, b):
            acc = bank(b, [P, HALF], F32, "acc2_%d_%d" % (mt, nh))
            codes, scales = T["qv", mt // 4]
            for g in range(2):
                cols = slice(HALF * g + P * (mt % 4), HALF * g + P * (mt % 4 + 1))
                moving = slice(HALF * g, HALF * (g + 1))
                nc.tensor.matmul_mx(
                    out=acc[:], lhsT=codes[:, cols].bitcast(FP8X4), lhsT_scale=scales[:, cols],
                    rhs=T["qp", nh][0][:, moving].bitcast(FP8X4), rhs_scale=T["qp", nh][1][:, moving],
                    start=(g == 0), stop=(g == 1),
                )
            T["acc2", mt, nh] = acc

        def add_extra(mt, nh):
            if ("sum", mt) not in T:
                T["sum", mt] = stage.tile([P, N], F32, name="sum%d" % mt, tag="summed", bufs=SUM_BUFS)
            cols = slice(HALF * nh, HALF * (nh + 1))
            nc.vector.scalar_tensor_tensor(
                out=T["sum", mt][:, cols], in0=T["acc2", mt, nh][:], scalar=gain1_cols[:, mt : mt + 1],
                in1=T["extra", mt // 4][:, mt % 4, cols], op0=MULT, op1=ADD,
            )

        def finish_y(mt, first, count, engine):
            if ("y", mt) not in T:
                T["y", mt] = stage.tile([P, N], F32, name="y%d" % mt, tag="y", bufs=Y_BUFS)
            cols = slice(HALF * first, HALF * (first + count))
            (nc.vector if engine == "V" else nc.gpsimd).tensor_tensor(out=T["y", mt][:, cols], in0=T["sum", mt][:, cols], in1=gain2_rows[:, cols], op=MULT)

        def store_y(mt, first, count):
            cols = slice(HALF * first, HALF * (first + count))
            nc.sync.dma_start(out=out_0[P * mt : P * (mt + 1), cols], in_=T["y", mt][:, cols])

        def round_y(mt, nh, engine):
            if ("yb", mt) not in T:
                T["yb", mt] = stage.tile([P, N], BF16, name="yb%d" % mt, tag="rounded", bufs=RND_BUFS)
            cols = slice(HALF * nh, HALF * (nh + 1))
            copy_on(engine, T["yb", mt][:, cols].rearrange("m (h p e) -> m h p e", h=2, e=2), T["y", mt][:, cols].rearrange("m (p h e) -> m h p e", h=2, e=2))

        def turn_y(mt, first, count, b):
            turned = bank(b, [P, count, 2, P], F32, "yt%d_%d" % (mt, first))
            words = T["yb", mt][:].bitcast(F32)
            for i in range(count):
                for h in range(2):
                    at = 2 * P * (first + i) + P * h
                    nc.tensor.transpose(turned[:, i, h, :], words[:, at : at + P], ident_f32[:])
            T["yt", mt, first] = turned

        def group_y(mt, first, count, engine):
            if ("gy", mt // 2) not in T:
                T["gy", mt // 2] = stage.tile([P, 2, 2, 4 * P], BF16, name="gy%d" % (mt // 2), tag="grouped_y", bufs=GY_BUFS, align_bytes=64)
            out = T["gy", mt // 2][:, first : first + count, mt % 2, :].bitcast(F32).rearrange("p g (m h) -> p g m h", h=2)
            copy_on(engine, out, T["yt", mt, first][:].rearrange("p g h m -> p g m h"))

        def quant_y(mt0, count, nh):
            cols = slice(P * (mt0 % 4), P * (mt0 % 4 + count))
            codes, scales = y_planes[mt0 // 4]
            nc.vector.quantize_mx(out=codes[:, nh, cols].bitcast(FP8X4), scales=scales[:, nh, cols], in_=T["gy", mt0 // 2][:, nh, mt0 % 2 : mt0 % 2 + count, :].rearrange("p i c -> p (i c)"))

        def store_codes(mt0, count, nh):
            words = out_1[nh].rearrange("p m t -> p (m t)").bitcast(I32)
            cols = slice(P * (mt0 % 4), P * (mt0 % 4 + count))
            nc.sync.dma_start(out=words[:, P * mt0 : P * (mt0 + count)], in_=y_planes[mt0 // 4][0][:, nh, cols].bitcast(I32))

        def store_scales(mh, queues):
            for q in range(4):
                queues[q].dma_start(
                    out=out_2[:, 4 * q : 4 * q + 4, HALF * mh : HALF * (mh + 1)].bitcast(I32).rearrange("g r c -> r g c"),
                    in_=y_planes[mh][1][32 * q : 32 * q + 4, :, :].bitcast(I32),
                )

        book_words = keep.tile([P, 2, 2 * M], U8, name="book_words", align_bytes=64)
        book_scales = keep.tile([P, 2, M], U8, name="book_scales", align_bytes=64)
        y_planes = []
        for mh in range(2):
            codes = keep.tile([P, 2, HALF], U32, name="y_codes%d" % mh, align_bytes=64)
            scales = keep.tile([P, 2, HALF], U8, name="y_scales%d" % mh, align_bytes=64)
            y_planes.append((codes, scales))
        ident_f32 = keep.tile([P, P], F32, name="ident_f32")
        ident_bf16 = keep.tile([P, P], BF16, name="ident_bf16")
        gain_rows = keep.tile([P, P], BF16, name="gain_rows")
        gain1_cols = keep.tile([P, 8], F32, name="gain1_cols")
        gain2_cols = keep.tile([P, 8], BF16, name="gain2_cols")
        gain2_rows = keep.tile([P, N], BF16, name="gain2_rows")
        weights_bf16 = keep.tile([P, 2, 4], BF16, name="weights_bf16")
        weights = keep.tile([P, 8], F32, name="weights")

        nc.sync.dma_start(out=gain2_cols[:], in_=gain2.rearrange("(p j) -> p j", j=8))
        nc.vector.memset(gain_rows[:].bitcast(I32), 0)
        nc.vector.memset(book_scales[:].bitcast(I32), 0)
        make_identity(nc, ident_f32[:])
        nc.scalar.dma_start(out=gain_rows[0:8, :], in_=gain1.rearrange("(j p) -> j p", p=P))
        nc.scalar.dma_start(out=weights_bf16[:], in_=user_weight.rearrange("(g p t) -> p g t", g=2, t=4))
        for q in range(4):
            nc.gpsimd.dma_start(
                out=book_scales[32 * q : 32 * q + 4, :, :].bitcast(I32),
                in_=codebook_scales[:, 4 * q : 4 * q + 4, :].bitcast(I32).rearrange("g r c -> r g c"),
            )
        nc.scalar.activation(out=ident_bf16[:], in_=ident_f32[:], func=COPY)

        def gains_turn(b):
            T["gain_cols"] = bank(b, [P, P], BF16, "gain_cols")
            nc.tensor.transpose(T["gain_cols"][:], gain_rows[:], ident_bf16[:])

        def gains_cols():
            nc.vector.tensor_copy(out=gain1_cols[:], in_=T["gain_cols"][:, 0:8])

        def widen_weights():
            nc.vector.tensor_copy(out=weights[:], in_=weights_bf16[:].rearrange("p g t -> p (g t)"))

        def gains_spread(b):
            T["spread"] = bank(b, [P, N], BF16, "spread")
            for j in range(8):
                nc.tensor.transpose(T["spread"][:, P * j : P * (j + 1)], gain2_cols[:, j : j + 1].to_broadcast([P, P]), ident_bf16[:])

        def gains_rows(engine):
            copy_on(engine, gain2_rows[:].rearrange("q (p j) -> q p j", j=8), T["spread"][:].rearrange("q (j p) -> q p j", j=8))

        gains_spread(0)
        load_channel(1)
        load_wide(1, 0)
        group_channel(1, 0, "S", 0, 256)
        gains_rows("V")
        group_channel(1, 1, "V", 0, 512)
        group_wide(1, 0, "V")
        group_channel(1, 0, "S", 256, 512)
        quant_channel(1, 0, 2)
        quant_wide(1, 0)
        stage1(1, 1, 0, 2, 1)
        stage1(1, 0, 0, 0, 2)
        stage1(1, 0, 0, 2, 3)
        stage1(1, 0, 0, 1, 4)
        stage1(1, 0, 0, 3, 5)
        load_wide(2, 0)
        group_wide(2, 0, "S")
        quant_wide(2, 0)
        load_channel(2)
        group_channel(2, 0, "V", 256, 512)
        load_wide(5, 0)
        group_channel(2, 1, "V", 0, 512)
        group_channel(2, 0, "S", 0, 256)
        quant_channel(2, 0, 2)
        stage1(2, 0, 0, 0, 2)
        load_channel(3)
        load_codebook(1)
        group_wide(5, 0, "S")
        quant_wide(5, 0)
        stage1(5, 1, 0, 3, 6)
        stage1(5, 1, 0, 2, 1)
        stage1(5, 1, 0, 1, 7)
        stage1(2, 0, 0, 2, 3)
        stage1(1, 1, 0, 3, 6)
        stage1(5, 1, 0, 0, 0)
        stage1(5, 0, 0, 3, 5)
        widen_weights()
        stage1(2, 0, 0, 3, 5)
        stage1(5, 0, 0, 2, 3)
        load_wide(3, 0)
        group_channel(3, 0, "V", 0, 256)
        stage1(2, 1, 0, 2, 1)
        stage1(2, 1, 0, 1, 7)
        load_wide(0, 0)
        stage1(2, 0, 0, 1, 4)
        stage1(1, 1, 0, 0, 0)
        group_channel(3, 0, "S", 256, 512)
        group_wide(3, 0, "V")
        quant_channel(3, 0, 1)
        stage1(5, 0, 0, 0, 2)
        quant_wide(3, 0)
        stage1(3, 0, 0, 0, 2)
        stage1(3, 0, 0, 3, 5)
        stage1(1, 1, 0, 1, 7)
        load_wide(4, 0)
        load_codebook(0)
        group_channel(3, 1, "S", 0, 512)
        quant_channel(3, 1, 1)
        stage1(3, 1, 0, 1, 7)
        stage1(3, 1, 0, 2, 1)
        stage1(3, 0, 0, 1, 4)
        stage1(2, 1, 0, 3, 6)
        stage1(2, 1, 0, 0, 0)
        stage1(3, 0, 0, 2, 3)
        group_wide(4, 0, "V")
        stage1(3, 1, 0, 3, 6)
        load_channel_half(0, 1)
        stage1(3, 1, 0, 0, 0)
        load_channel_half(0, 0)
        group_wide(0, 0, "S")
        quant_wide(0, 0)
        quant_wide(4, 0)
        stage1(4, 0, 0, 3, 5)
        stage1(4, 1, 0, 3, 6)
        stage1(4, 0, 0, 1, 4)
        stage1(5, 0, 0, 1, 4)
        stage1(4, 0, 0, 2, 3)
        stage1(4, 0, 0, 0, 2)
        group_channel(0, 0, "V", 0, 256)
        group_channel(0, 1, "S", 0, 512)
        load_wide(3, 1)
        group_channel(0, 0, "V", 256, 512)
        quant_channel(0, 1, 1)
        stage1(4, 1, 0, 1, 7)
        stage1(4, 1, 0, 2, 1)
        stage1(0, 1, 0, 0, 0)
        stage1(0, 1, 0, 3, 6)
        stage1(0, 1, 0, 2, 1)
        stage1(4, 1, 0, 0, 0)
        stage1(0, 1, 0, 1, 7)
        quant_channel(0, 0, 1)
        stage1(0, 0, 0, 0, 2)
        stage1(0, 0, 0, 2, 3)
        stage1(0, 0, 0, 1, 4)
        stage1(0, 0, 0, 3, 5)
        load_wide(2, 1)
        group_wide(3, 1, "S")
        load_precoder(0)
        group_wide(2, 1, "V")
        quant_wide(3, 1)
        weigh(1, 0, 3, "S")
        weigh(1, 0, 0, "S")
        weigh(1, 0, 1, "S")
        weigh(0, 0, 2, "V")
        load_wide(1, 1)
        stage1(3, 0, 1, 0, 6)
        weigh(0, 0, 3, "S")
        turn_precoder(0, 1, 1, 0)
        group_precoder(0, 1, 1, "S")
        turn_precoder(0, 1, 0, 3)
        stage1(3, 0, 1, 2, 7)
        load_wide(5, 1)
        quant_wide(2, 1)
        stage1(2, 0, 1, 2, 7)
        turn_precoder(0, 0, 1, 5)
        turn_precoder(0, 0, 0, 0)
        group_precoder(0, 1, 0, "S")
        group_wide(1, 1, "V")
        stage1(2, 0, 1, 0, 6)
        stage1(2, 0, 1, 3, 3)
        stage1(3, 0, 1, 3, 3)
        weigh(0, 0, 1, "S")
        stage1(2, 1, 1, 2, 4)
        weigh(0, 0, 0, "S")
        stage1(2, 0, 1, 1, 2)
        stage1(3, 1, 1, 2, 4)
        stage1(3, 0, 1, 1, 2)
        group_wide(5, 1, "V")
        quant_wide(1, 1)
        stage1(1, 0, 1, 2, 7)
        stage1(1, 1, 1, 2, 4)
        group_precoder(0, 0, 0, "S")
        load_wide(0, 1)
        stage1(1, 0, 1, 3, 3)
        load_wide(4, 1)
        group_wide(0, 1, "S")
        quant_wide(5, 1)
        stage1(1, 0, 1, 1, 2)
        stage1(5, 0, 1, 2, 7)
        stage1(5, 0, 1, 0, 6)
        stage1(5, 0, 1, 3, 3)
        stage1(1, 0, 1, 0, 6)
        group_precoder(0, 0, 1, "S")
        group_vw(0, 0, "S", 0, 512)
        group_wide(4, 1, "V")
        stage1(2, 1, 1, 3, 0)
        stage1(5, 0, 1, 1, 2)
        quant_wide(4, 1)
        stage1(4, 0, 1, 2, 7)
        stage1(4, 0, 1, 3, 3)
        quant_wide(0, 1)
        stage1(4, 0, 1, 1, 2)
        stage1(0, 0, 1, 1, 2)
        stage1(0, 0, 1, 2, 7)
        weigh(0, 1, 1, "S")
        quant_precoder(0)
        stage1(0, 0, 1, 3, 3)
        weigh(0, 1, 3, "S")
        stage1(0, 0, 1, 0, 6)
        weigh(0, 1, 2, "V")
        load_precoder(1)
        stage1(4, 0, 1, 0, 6)
        quant_vw(0, 0, 1)
        turn_precoder(1, 1, 0, 5)
        weigh(0, 1, 0, "V")
        turn_precoder(1, 1, 1, 7)
        group_precoder(1, 1, 0, "S")
        gains_turn(2)
        stage1(3, 1, 1, 3, 0)
        group_precoder(1, 1, 1, "S")
        gains_cols()
        turn_precoder(1, 0, 0, 3)
        group_vw(0, 1, "V", 256, 512)
        group_vw(0, 1, "V", 0, 256)
        quant_vw(0, 1, 1)
        turn_precoder(1, 0, 1, 6)
        stage1(4, 1, 1, 2, 4)
        group_precoder(1, 0, 0, "S")
        group_precoder(1, 0, 1, "S")
        quant_precoder(1)
        stage1(4, 1, 1, 1, 2)
        stage1(4, 1, 1, 3, 0)
        stage1(0, 1, 1, 2, 4)
        stage1(0, 1, 1, 3, 0)
        load_extra(0)
        stage2(2, 0, 5)
        stage2(1, 0, 7)
        weigh(1, 0, 2, "S")
        add_extra(2, 0)
        stage2(2, 1, 3)
        finish_y(2, 0, 1, "G")
        group_vw(1, 0, "S", 0, 512)
        stage2(1, 1, 6)
        stage1(5, 1, 1, 2, 4)
        add_extra(1, 0)
        stage1(1, 1, 1, 3, 0)
        add_extra(2, 1)
        finish_y(2, 1, 1, "V")
        finish_y(1, 0, 1, "G")
        add_extra(1, 1)
        stage2(3, 0, 1)
        weigh(1, 1, 2, "S")
        add_extra(3, 0)
        round_y(2, 1, "S")
        finish_y(1, 1, 1, "V")
        finish_y(3, 0, 1, "G")
        stage2(3, 1, 5)
        add_extra(3, 1)
        stage1(3, 1, 1, 1, 2)
        stage1(5, 1, 1, 3, 0)
        stage1(0, 1, 1, 1, 2)
        weigh(1, 1, 3, "V")
        finish_y(3, 1, 1, "V")
        round_y(2, 0, "S")
        stage1(5, 1, 1, 1, 2)
        stage1(2, 1, 1, 1, 2)
        load_extra(1)
        round_y(1, 0, "S")
        round_y(1, 1, "S")
        stage1(1, 1, 1, 1, 2)
        weigh(1, 1, 1, "S")
        quant_vw(1, 0, 1)
        store_y(2, 0, 2)
        stage1(3, 1, 1, 0, 7)
        stage1(5, 1, 1, 0, 7)
        stage1(4, 1, 1, 0, 7)
        stage1(1, 1, 1, 0, 7)
        stage1(2, 1, 1, 0, 7)
        stage1(0, 1, 1, 0, 7)
        weigh(1, 1, 0, "S")
        group_vw(1, 1, "V", 256, 512)
        stage2(0, 0, 3)
        group_vw(1, 1, "S", 0, 256)
        store_y(1, 0, 2)
        stage2(0, 1, 4)
        add_extra(0, 1)
        turn_y(2, 0, 2, 6)
        quant_vw(1, 1, 1)
        turn_y(1, 0, 2, 1)
        stage2(5, 0, 5)
        round_y(3, 1, "S")
        add_extra(0, 0)
        stage2(5, 1, 0)
        store_y(3, 0, 2)
        finish_y(0, 1, 1, "V")
        stage2(7, 0, 2)
        add_extra(5, 0)
        group_y(1, 0, 2, "S")
        group_y(2, 0, 2, "S")
        round_y(3, 0, "S")
        finish_y(0, 0, 1, "G")
        round_y(0, 1, "S")
        round_y(0, 0, "S")
        store_y(0, 0, 2)
        stage2(7, 1, 7)
        add_extra(5, 1)
        stage2(4, 1, 4)
        finish_y(5, 0, 1, "V")
        finish_y(5, 1, 1, "G")
        turn_y(3, 0, 2, 1)
        store_y(5, 0, 2)
        round_y(5, 0, "S")
        add_extra(7, 1)
        turn_y(0, 0, 2, 3)
        group_y(0, 0, 2, "S")
        stage2(4, 0, 6)
        round_y(5, 1, "S")
        stage2(6, 0, 5)
        add_extra(7, 0)
        stage2(6, 1, 0)
        finish_y(7, 1, 1, "V")
        store_y(7, 1, 1)
        round_y(7, 1, "S")
        finish_y(7, 0, 1, "G")
        store_y(7, 0, 1)
        add_extra(4, 0)
        add_extra(4, 1)
        finish_y(4, 0, 1, "V")
        finish_y(4, 1, 1, "G")
        store_y(4, 0, 2)
        add_extra(6, 1)
        add_extra(6, 0)
        quant_y(0, 2, 0)
        turn_y(5, 0, 2, 7)
        quant_y(0, 2, 1)
        round_y(7, 0, "S")
        group_y(3, 0, 2, "S")
        quant_y(2, 2, 0)
        store_codes(0, 4, 0)
        round_y(4, 0, "S")
        quant_y(2, 2, 1)
        store_codes(0, 4, 1)
        finish_y(6, 0, 1, "V")
        finish_y(6, 1, 1, "V")
        round_y(6, 1, "V")
        round_y(4, 1, "S")
        turn_y(4, 0, 2, 2)
        turn_y(7, 0, 1, 3)
        group_y(5, 0, 2, "S")
        round_y(6, 0, "S")
        group_y(4, 0, 2, "S")
        group_y(7, 0, 1, "V")
        quant_y(4, 2, 1)
        quant_y(4, 2, 0)
        turn_y(7, 1, 1, 6)
        turn_y(6, 0, 2, 4)
        group_y(7, 1, 1, "S")
        quant_y(7, 1, 1)
        store_scales(0, [nc.sync] * 4)
        store_y(6, 0, 2)
        store_codes(4, 2, 0)
        quant_y(7, 1, 0)
        group_y(6, 0, 2, "S")
        store_codes(4, 2, 1)
        quant_y(6, 1, 0)
        store_codes(6, 2, 0)
        quant_y(6, 1, 1)
        store_scales(1, [nc.sync] * 4)
        store_codes(6, 2, 1)
